import numpy as np, ml_dtypes
CORES = [1,5,17,21,33,37,49,53]
N = 8
BF = ml_dtypes.bfloat16
W, E, S, M, RO, DB, DC, CM, EX = 2048, 256, 8, 8, 3, 3, 2, 10, 5
def pack(x, p, r, z):
    return {"x0": np.ascontiguousarray(x.reshape(N, 128, W)).astype(np.float32).astype(BF), "lk": np.ascontiguousarray(p.reshape(N, 128, W)).astype(np.int32),
            "rd": np.ascontiguousarray(r.reshape(N, 128, E)).astype(np.int32), "z0": np.ascontiguousarray(z.reshape(N, 128, E)).astype(np.float32).astype(BF)}
def parts(rng):
    lev = np.repeat(rng.choice(np.array([24, 60, 120, 190, 255]), (N, 8, 1, 8)), W // 8, axis=3)
    x = (rng.random((N, 8, 16, W)) * (lev + 1)).astype(np.int64) * (rng.random((N, 8, 1, W)) > 0.0625)
    share = np.stack([rng.permutation(np.array([0.1, 0.1, 0.3, 0.3, 0.6, 0.6, 0.9, 0.95])) for q in range(N)]).reshape(N, 8, 1, 1)
    to = np.where(rng.random((N, 8, 16, W)) < 0.5, S * rng.integers(0, E, (N, 8, 16, W)), rng.integers(0, W, (N, 8, 16, W)))
    p = np.where(rng.random((N, 8, 16, W)) < share, to, W)
    near = rng.integers(0, 8, (N, 8, 1, E)) * (W // 8) + rng.integers(0, W // 8, (N, 8, 16, E))
    r = np.where(rng.random((N, 8, 1, E)) < 0.5, near, rng.integers(0, W, (N, 8, 16, E)))
    z = (rng.random((N, 8, 16, E)) * (rng.choice(np.array([40, 120, 255]), (N, 8, 1, E)) + 1)).astype(np.int64)
    return x, p, r, z
def setup_inputs(rng):
    return pack(*parts(rng))
def setup_inputs_spread(rng):
    x = np.minimum((np.exp2(9 * rng.random((N, 8, 1, W))) * rng.random((N, 8, 16, W))).astype(np.int64), 255)
    z = np.minimum((np.exp2(9 * rng.random((N, 8, 1, E))) * rng.random((N, 8, 16, E))).astype(np.int64), 255)
    to = np.minimum((W * rng.random((N, 8, 16, W)) ** 3).astype(np.int64), W - 1)
    p = np.where(rng.random((N, 8, 16, W)) < rng.random((N, 8, 16, 1)), to, W)
    r = np.minimum((W * rng.random((N, 8, 16, E)) ** rng.choice(np.array([1.0, 2.0, 4.0]), (N, 8, 1, 1))).astype(np.int64), W - 1)
    return pack(x, p, r, z)
def setup_inputs_ends(rng):
    kind = rng.integers(0, 4, (N, 8, 1, W)); el = 255 * rng.integers(0, 2, (N, 8, 16, W))
    x = np.where(kind == 0, 0, np.where(kind == 1, 255, el))
    v = rng.permutation(np.array([0, 255] * 4)); x[..., 0] = v[None, :, None]; x[..., W - 1] = 255 - v[None, :, None]
    x[..., W - 2] = 255 - v[None, :, None]; x[:, :, 15, W - 2] = np.where(v == 0, 254, 1)[None, :]
    p = np.where(rng.random((N, 8, 16, W)) < 0.2, rng.integers(0, W, (N, 8, 16, W)), W * (rng.random((N, 8, 16, W)) < 0.65))
    p[..., 0] = W; p[:, :, 0, 0] = W - 2; p[:, :, [1, 15], 0] = W - 1; p[..., W - 1] = W; p[:, :, [0, 15], W - 1] = 0
    way = rng.integers(0, 4, (N, 8, 1, E)); way[..., 0] = 0; way[..., E - 2] = 0; way[..., E - 1] = 1
    end = (W - 1) * rng.integers(0, 2, (N, 8, 16, E)); some = np.where(rng.random((N, 8, 16, E)) < 0.5, end, rng.integers(0, W, (N, 8, 16, E)))
    r = np.where(way == 0, 0, np.where(way == 1, W - 1, np.where(way == 2, end, some)))
    z = 255 * np.where(rng.random((N, 8, 1, E)) < 0.5, rng.integers(0, 2, (N, 8, 1, E)), rng.integers(0, 2, (N, 8, 16, E)))
    return pack(x, p, r, z)
def setup_inputs_corners(rng):
    x, p, r, z = parts(rng); gt = rng.permutation(8); H = W // 2
    for g in range(8):
        m = int(gt[g])
        if m < 2:
            x[:, g, :, 1::2] = 128
            h = rng.integers(0, 17, (N, 1, H)) if m == 0 else rng.choice(np.array([EX, EX + 1, CM - 1, CM]), (N, 1, H))
            up = np.argsort(rng.random((N, 16, H)), axis=1) < h; one = rng.random((N, 16, H)) < (0.5 if m == 0 else 2.0)
            x[:, g, :, 0::2] = np.where(up, np.where(one, 128, rng.integers(128, 256, (N, 16, H))), np.where(one, 127, rng.integers(0, 128, (N, 16, H))))
            p[:, g] = np.where(rng.random((N, 16, W)) < 0.4, 2 * rng.integers(0, H, (N, 16, W)), W)
            r[:, g] = 2 * rng.integers(0, H, (N, 16, E)) + 1
        elif m == 2:
            full = rng.integers(0, W, (N, 16, W)); p[:, g] = np.where((np.arange(N) % 2 == 0)[:, None, None], full, W)
        elif m == 3:
            r[:, g] = S * np.arange(E)[None, :] + (np.arange(16) % S)[:, None]
            p[:, g] = np.where(rng.random((N, 16, W)) < 0.5, S * (np.arange(W) // S), W)
            x[:, g, :, 0::S] = x[:, g, :, 0::S] * (rng.random((N, 1, E)) < 0.5)
        elif m == 4:
            x[:, g] = x[:, g] * (rng.random((N, 1, W)) < 0.3); z[:, g] = z[:, g] * (rng.random((N, 1, E)) < 0.5)
            x[:, g, :15, 0::S] = 0; x[:, g, 15, 0::S] = rng.integers(1, 256, (N, E)) * (rng.random((N, E)) < 0.5)
            p[:, g] = np.where(rng.random((N, 16, W)) < 0.5, rng.integers(0, W, (N, 16, W)), W)
        elif m == 5:
            p[:, g] = rng.choice(np.array([0, W - 1, W]), (N, 16, W))
            r[:, g] = np.where(rng.random((N, 16, E)) < 0.5, (W - 1) * rng.integers(0, 2, (N, 16, E)), r[:, g])
        elif m == 6:
            p[:, g] = np.where(rng.random((N, 16, W)) < 0.5, rng.integers(0, W, (N, 16, W)), W)
            x[:, g, :, 0::S] = np.maximum(x[:, g, :, 0::S], 1)
            for b in range(N):
                a = S * rng.permutation(E) + 1; d = S * rng.permutation(E) + S - 1
                high = rng.integers(128, 256, (16, E)); low = rng.integers(1, 100, (16, E))
                x[b, g][:, a] = high if b % 2 == 0 else low
                x[(b + DC) % N, g][:, d] = low if b % 2 == 0 else high
                up = np.argsort(rng.random((16, E)), axis=0) < rng.integers(1, 16, (1, E))
                p[b, g][:, a] = np.where(up, d[None, :], W)
                r[(b - DB) % N, g] = a[None, :]
        else:
            p[:, g] = W; p[:, g, 0] = S * rng.integers(0, E, (N, W)); p[:, g, 15] = rng.integers(0, W, (N, W))
    return pack(x, p, r, z)
def setup_inputs_crowd(rng):
    x, p, r, z = parts(rng); gt = rng.permutation(8)
    for g in range(8):
        m = int(gt[g]); i = int(rng.integers(1, E - 1)); b = S * i + (0 if m in (0, 3, 5, 6) else S - 1)
        a = (0, W - 1, S * (i - 1) + 1, S * i + 1)[m % 4]
        x[:, g, :, a] = rng.integers(128, 256, (N, 16)); x[:, g, :, b] = rng.integers(1, 100, (N, 16))
        p[:, g, :, a] = W; rows = rng.permutation(16)[:5]; p[:, g, rows, a] = b
        r[:, g] = a
        if m >= 4: r[:, g, :, (0, E - 1, 1, i)[m % 4]] = rng.integers(0, W, (N, 16))
    return pack(x, p, r, z)
def check_inputs(d):
    bad = []
    for k, lo, hi in (("x0", 0, 255), ("lk", 0, W), ("rd", 0, W - 1), ("z0", 0, 255)):
        v = np.asarray(d[k]).astype(np.float64)
        if not (np.min(v) >= lo and np.max(v) <= hi): bad.append("range of " + k)
        if np.any(v != np.floor(v)): bad.append("whole numbers of " + k)
        if np.any((v == 0) & np.signbit(v)): bad.append("-0.0 in " + k)
    return bad
def reference(x0, lk, rd, z0):
    X = x0.astype(np.float32).astype(np.int64).reshape(N, 8, 16, W); P = lk.astype(np.int64).reshape(N, 8, 16, W)
    R = rd.astype(np.int64).reshape(N, 8, 16, E); z = z0.astype(np.float32).astype(np.int64).reshape(N, 8, 16, E)
    bi = (np.arange(N) + DB) % N; ci = (np.arange(N) + DB + DC) % N; lane = np.arange(E)
    q = np.zeros((N, 8, E), np.int64) + S * lane
    rows = np.arange(16)[None, None, :, None]; ai = np.arange(N)[:, None, None]; gi = np.arange(8)[None, :, None]
    for t in range(RO):
        XB = X[bi]; PB = P[bi]; flat = R.reshape(N, 8, 1, 16 * E)
        L = np.take_along_axis(PB, R, 3)
        xs = np.take_along_axis(XB, flat, 3).reshape(N, 8, 16, 16, E)
        free = (L == W)[:, :, None]
        top = np.max(np.where(free, xs, -1), axis=3); low = np.min(np.where(free, xs, 256), axis=3)
        y = np.where(top >= 0, (top + low) >> 1, z)
        XC = X[ci]
        orphan = ~np.any(np.take_along_axis(XC, q[:, :, None, :], 3) != 0, axis=2)
        q = np.where(orphan, S * lane + (y[:, :, 0] & 7), q)
        np.put_along_axis(XC, q[:, :, None, :], y, 3)
        es = np.take_along_axis(XC, np.minimum(L, W - 1).reshape(N, 8, 1, 16 * E), 3).reshape(N, 8, 16, 16, E)
        yk = y[:, :, :, None, :]
        n = np.add.reduce((es >= yk).astype(np.int64), axis=2); dist = np.add.reduce(np.abs(es - yk), axis=2)
        com = (L < W) & (n >= CM); late = (L < W) & (n <= EX); settled = com | late
        ks = np.where(np.any(settled, axis=2), np.argmax(np.where(settled, dist, -1), axis=2), 15); kk = ks[:, :, None, :]
        com = np.take_along_axis(com, kk, 2)[:, :, 0]; late = np.take_along_axis(late, kk, 2)[:, :, 0]
        Ls = np.take_along_axis(L, kk, 2)[:, :, 0]; cell = np.take_along_axis(R, kk, 2)[:, :, 0]
        ev = np.take_along_axis(es, ks[:, :, None, None, :], 3)[:, :, :, 0]
        a, g, e = np.nonzero(late); XC[a, g, :, Ls[a, g, e]] = 0
        X[ci] = XC
        best = np.full((N, 8, W), E, np.int64); np.minimum.at(best, (ai, gi, cell), lane + np.zeros_like(cell))
        win = np.take_along_axis(best, cell, 2) == lane
        XB = X[bi]; a, g, e = np.nonzero(win & com); c = cell[a, g, e]
        XB[a, g, :, c] = (XB[a, g, :, c] + ev[a, g, :, e]) >> 1
        X[bi] = XB
        if t < RO - 1:
            a, g, e = np.nonzero(win & (com | late)); PB[a, g, ks[a, g, e], cell[a, g, e]] = W
            a, g, e = np.nonzero(win); PB[a, g, (e + t) % 16, cell[a, g, e]] = q[a, g, e]
            P[bi] = PB
        v = np.where((rows == kk) & com[:, :, None], L, R) + M * np.where(orphan[:, :, None], 255 - y, y) + 1
        R = np.where(v >= W, v - W, v); z = y
    return {"xo": X.reshape(N, 128, W).astype(np.float32).astype(BF), "ro": R.reshape(N, 128, E).astype(np.float32), "zo": z.reshape(N, 128, E).astype(np.float32).astype(BF)}

@@ -1,0 +1,622 @@
+from concourse.mybir import AluOpType, ActivationFunctionType
+
+N, W, E, RO, DB, DC = 8, 2048, 256, 3, 3, 2
+XO = 16
+DUM = 2064
+BIG = 4096.0
+BV = float(1 << 22)
+MAGIC = 12582912.0
+CH = [(0, 64), (64, 128), (128, 192), (192, 256)]
+PENG = ["dve", "act", "act", "act"]
+XENG = ["act"] * 5
+YCUT = 192
+ECH = [(0, 64, "dve"), (64, 128, "act"), (128, 192, "dve"), (192, 256, "act")]
+EACT4 = []
+EACT5 = []
+EL4, EL5 = [], []
+FIRST = 3000.0
+CYC, GAT, SCA, PEC, FIX, HOP, FAR, BW, WIN = 1.04, 1.56, 3.8, 0.53, 30.0, 60.0, 2000.0, 60.0, 0.25
+
+F, H, B, I, U = "float32", "float16", "bfloat16", "int32", "uint16"
+BUFS = [
+    ("X", 2336, B), ("P", 2320, F), ("lki", 2048, I), ("rdi", 256, I), ("r0s", 256, U), ("z0s", 256, B), ("zl", 256, B),
+    ("R1", 512, H), ("G32", 4096, F), ("G16", 4096, H), ("fB", 256, H), ("uw", 512, H),
+    ("ix", 256, F), ("ixu", 256, U), ("xg", 4096, B), ("smx", 4096, B), ("smn", 4096, B), ("zz", 256, B), ("Lf", 256, F),
+    ("xq", 256, H), ("sm", 192, F), ("si", 64, I), ("su", 64, U), ("qh", 32, H), ("eg", 4096, B), ("ge", 4096, B), ("ab", 4096, B),
+    ("tB", 256, F), ("km", 256, F), ("S", 256, F), ("sp", 256, H), ("rep", 256, H), ("a123", 768, B),
+    ("key", 256, H), ("cr", 256, H), ("EE", 16 * 272, B), ("sc", 256, F), ("sc4", 256, F), ("U8", 256, B), ("Qd", 256, F),
+    ("oP", 256, F), ("oX", 256, B), ("bP", 256, F), ("aa", 256, F), ("v2", 256, F), ("vi", 256, I), ("vj", 256, I),
+    ("rol", 256, U), ("rof", 256, F), ("zol", 256, B), ("Rl3", 256, U),
+    ("pj", 144, F), ("jg", 128, F), ("jk", 256, F), ("jj", 256, F), ("pi", 8, I), ("col", 16, F), ("km16", 16, F), ("ltB", 16, F),
+    ("id32", 128, F), ("idb", 128 * 5, B), ("idh", 128 * 5, H), ("onh", 128 * 5, H),
+    ("dg32", 2048, F), ("dg16", 2048, H), ("tri", 2048, B), ("oto", 144, H), ("kto", 144, H), ("sto", 144, B),
+    ("D0", 256, F), ("OFF", 256, B), ("MB", 512, B), ("rs0", 1024, B), ("rb", 1024, B), ("pot", 256, B), ("il", 80, F), ("q0", 16, U),
+    ("Gn", 32, B), ("cV", 256, B), ("ct", 512, B), ("ch", 256, H), ("tmp", 256, F),
+]
+for _t in range(RO):
+    BUFS += [("%s%d" % (_n, _t), _c, _d) for _n, _c, _d in [
+        ("Rl", 256, U), ("ys", 256, B), ("yl", 256, B), ("qu", 16, U), ("ql", 16, U), ("ks", 16, U), ("kl", 16, U),
+        ("ns", 512, B), ("nl", 512, B), ("ws", 16, U), ("wl", 16, U)]]
+BUFS += [("XC", 2320, B), ("Ls", 256, U), ("orow", 256, B), ("hs", 768, H), ("es", 256, B), ("key5", 256, H), ("cr5", 256, H),
+         ("EE5", 16 * 272, B), ("EA", 16 * 272, B), ("EA5", 16 * 272, B), ("cl", 32, F), ("cl5", 32, F), ("onBb", 128, B), ("L1", 256, F)]
+SCRATCH = {}
+PLACE = {}
+for _n, _c, _d in BUFS:
+    if _c >= 1024:
+        SCRATCH[_n] = ("sbuf", [128, _c], _d)
+        PLACE[_n] = (_n, 0, _c)
+    else:
+        _p = "all_" + _d
+        _o = SCRATCH[_p][1][1] if _p in SCRATCH else 0
+        SCRATCH[_p] = ("sbuf", [128, _o + (_c + 15) // 16 * 16], _d)
+        PLACE[_n] = (_p, _o, _c)
+for _t in range(8):
+    SCRATCH["ps%d" % _t] = ("psum", [128, 512], F)
+    PLACE["ps%d" % _t] = ("ps%d" % _t, 0, 512)
+
+SEMAPHORES = ["dve", "act", "pe", "pool", "sent", "st", "ld0", "ld1", "ld2", "ld3", "ld4", "mr", "mz", "mro", "mzo", "mx", "sx"] + \
+    ["m%s%d" % (k, t) for t in range(RO) for k in ("y", "q", "k", "n", "w")]
+
+
+def rank_program(g, core, T, topo):
+    rank = T.rank_of(core)
+    if rank is None:
+        return
+    A = AluOpType
+    AF = ActivationFunctionType
+    ops = []
+    acc = {}
+
+    def v(name, a=0, b=None, s=1):
+        p, o, n = PLACE[name]
+        return (p, o + a, o + (n if b is None else b), s, name)
+
+    def ind(win, off):
+        return ("*", win, off)
+
+    def ap(x):
+        if x[0] == "*":
+            return ap(x[1]).indirect(ap(x[2]))
+        return T[x[0]][:, x[1]:x[2]] if x[3] == 1 else T[x[0]][:, x[1]:x[2]:x[3]]
+
+    def arg(x):
+        return ap(x) if isinstance(x, tuple) else x
+
+    def rec(q, fn, reads, writes, tok=None, kind=None):
+        k = len(ops)
+        deps, order = set(), set()
+        rs, ws = [], []
+        o = writes[0] if writes else None
+        full = [x for x in reads if isinstance(x, tuple) and (x[0] == "*" or x[2] - x[1] > 1)]
+        cost, lat = 60.0, 0.0
+        if tok is not None:
+            x = reads[0] if reads else (o if o else None)
+            size = 128 * (x[2] - x[1]) * (4 if SCRATCH[x[0]][2] in (F, I) else 2)
+            if q == "land":
+                cost, lat = 0.0, FAR + size / BW
+                order.add(k - 1)
+            elif q == "pool":
+                cost, lat = 400.0, FAR + size / BW
+            else:
+                cost, lat = (size / 250.0, 1800.0) if q == "sync" else (60.0, 1800.0 + size / 250.0)
+        elif q == "pe":
+            cost = max(64, len(range(o[1], o[2], o[3]))) * PEC * (4 if SCRATCH[reads[0][0]][2] == F else 1)
+        elif o[0] == "*":
+            cost = 55 + 16 * (o[2][2] - o[2][1]) * SCA * CYC
+        else:
+            n = len(range(o[1], o[2], o[3]))
+            if full and full[0][0] == "*":
+                cost = 55 + n * GAT * CYC
+            else:
+                per = 2.0 if q == "pool" else 1.0
+                if q == "dve" and kind == "tt":
+                    per = 1.0 if any(SCRATCH[x[0]][0] == "psum" for x in full) else 2.0
+                elif q == "dve" and all(SCRATCH[x[0]][2] in (H, B, U) for x in full + [o]):
+                    per = 0.5
+                cost = FIX + max(64, n * per) * CYC + (100 if q == "pool" else 0)
+        for x in reads:
+            if isinstance(x, tuple):
+                rs += [x[1], x[2]] if x[0] == "*" else [x]
+        for x in writes:
+            if x[0] == "*":
+                ws.append(x[1])
+                rs.append(x[2])
+            else:
+                ws.append(x)
+        for lst, wr in ((rs, False), (ws, True)):
+            for x in lst:
+                if SCRATCH[x[0]][0] == "psum":
+                    ep = acc.setdefault(x[4], [None, [], []])
+                    if ep[0] != q:
+                        ep[0], ep[1], ep[2] = q, [], ep[1]
+                    deps.update(a[2] for a in ep[2])
+                    if q == "pe":
+                        order.update(a[2] for a in ep[1][-1:])
+                    else:
+                        deps.update(a[2] for a in ep[1] if (wr or a[3]) and a[0] < x[2] and x[1] < a[1] and a[2] != k)
+                    ep[1].append((x[1], x[2], k, wr))
+                    continue
+                rd_, wr_ = acc.setdefault(x[4], ([], []))
+                deps.update(a[2] for a in (rd_ + wr_ if wr else wr_) if a[0] < x[2] and x[1] < a[1] and a[2] != k)
+                if wr and x[3] == 1:
+                    rd_[:] = [a for a in rd_ if not (x[1] <= a[0] and a[1] <= x[2])]
+                    wr_[:] = [a for a in wr_ if not (x[1] <= a[0] and a[1] <= x[2])]
+                (wr_ if wr else rd_).append((x[1], x[2], k))
+        if q == "sync":
+            order.update(acc.get("*sync", []))
+            acc["*sync"] = [k]
+        ops.append({"q": q, "fn": fn, "deps": deps, "tok": tok, "order": order, "cost": cost, "lat": lat})
+
+    def inturn(name):
+        name = "*" + name + ops[-1]["q"]
+        ops[-1]["order"].update(acc.get(name, []))
+        acc[name] = [len(ops) - 1]
+
+    def cp(out, in_):
+        rec("dve", lambda: g.vector.tensor_copy(ap(out), ap(in_)), [in_], [out])
+
+    def tt(out, a, b, op):
+        rec("dve", lambda: g.vector.tensor_tensor(ap(out), ap(a), ap(b), op), [a, b], [out], kind="tt")
+
+    def ts(out, a, s1, op0, s2=None, op1=None):
+        if op1 is None:
+            rec("dve", lambda: g.vector.tensor_scalar(ap(out), ap(a), arg(s1), None, op0), [a, s1], [out])
+        else:
+            rec("dve", lambda: g.vector.tensor_scalar(ap(out), ap(a), arg(s1), arg(s2), op0, op1), [a, s1, s2], [out])
+
+    def scan(out, d0, d1, op0, op1):
+        rec("dve", lambda: g.vector.tensor_tensor_scan(ap(out), ap(d0), ap(d1), 0.0, op0, op1), [d0, d1], [out])
+
+    def ms(out, c):
+        rec("dve", lambda: g.vector.memset(ap(out), c), [], [out])
+
+    def act(out, in_, func, bias=0.0, scale=1.0):
+        rec("act", lambda: g.scalar.activation(ap(out), ap(in_), func, bias=arg(bias), scale=arg(scale)), [in_, bias, scale], [out])
+
+    def mm(o, l, r, start, stop):
+        rec("pe", lambda: g.tensor.matmul(ap(o), ap(l), ap(r), start, stop), [l, r], [o])
+
+    def mms(lst):
+        for i, (o, l, r) in enumerate(lst):
+            mm(o, l, r, i == 0, i == len(lst) - 1)
+
+    def iota(out, pat, base, cm):
+        if SCRATCH[out[0]][2] == I:
+            rec("pool", lambda: g.iota(ap(out), pat, base, cm), [], [out])
+        else:
+            rec("pool", lambda: g.iota(ap(out), pat, base, cm, allow_small_or_imprecise_dtypes=True), [], [out])
+
+    def gather(eng, out, win, off):
+        if eng == "act":
+            act(out, ind(win, off), AF.Copy)
+        else:
+            cp(out, ind(win, off))
+
+    total = {}
+
+    def dma(q, out, in_, reads, writes, sem):
+        e = g.sync if q == "sync" else g.scalar
+        total[sem] = total.get(sem, 0) + 16
+        rec(q, lambda: e.dma_start(out, in_).then_inc(T.sem[sem], 16), reads, writes, tok=(sem, total[sem]))
+
+    def msg(src, hop, dst, sem, part=None, own="sent"):
+        to = T.cores[(rank + hop) % N]
+        frm = T.cores[(rank - hop) % N]
+        rid, pid, _ = topo.addr(to)
+
+        def pick(a, b):
+            e = topo.engines(a, b)
+            return e if part is None else e[part::2]
+        mask = sum(1 << e for e in pick(core, to))
+        total[own] = total.get(own, 0) + len(pick(core, to))
+        total[sem] = len(pick(frm, core))
+        rec("pool", lambda: g.remote_dma(ap(dst), ap(src), T.sem[sem], T.sem[own], pid, rid, mask), [src], [],
+            tok=(own, None if own == "sent" else total[own]))
+        rec("land", None, [], [dst], tok=(sem, total[sem]))
+
+    def ps(b, a=0, e=512, s=1):
+        return v("ps%d" % b, a, e, s)
+
+    def col(j):
+        return v("col", j, j + 1)
+
+    def blk(name, k):
+        return v(name, 128 * k, 128 * k + 128)
+
+    def wnd(name, k):
+        return v(name, 15 - k, 143 - k)
+
+    Xc = v("X", XO, 2336)
+    XC = v("XC")
+    Pc = v("P", 0, W)
+    R1 = v("R1", 0, 256)
+    idb, idhalf, idn, id8, ido = [blk("idb", j) for j in range(5)]
+    idh, idhn, idB, idN, M1 = [blk("idh", j) for j in range(5)]
+    onh, onB, onN, shf, onn = [blk("onh", j) for j in range(5)]
+    cq, c0 = v("ct", 0, 256), v("ct", 256, 512)
+    il1, il8, il16, ilq, ild = [v("il", 16 * j, 16 * j + 16) for j in range(5)]
+
+    dma("sync", ap(v("rdi")), T.rd[:], [], [v("rdi")], "ld0")
+    dma("act", ap(v("z0s")), T.z0[:], [], [v("z0s")], "ld1")
+    dma("sync", ap(v("lki", 0, 1024)), T.lk[:, 0:1024], [], [v("lki", 0, 1024)], "ld2")
+    dma("sync", ap(v("lki", 1024, 2048)), T.lk[:, 1024:2048], [], [v("lki", 1024, 2048)], "ld3")
+    dma("sync", ap(v("X", XO, XO + W)), T.x0[:], [], [v("X", XO, XO + W)], "ld4")
+    iota(v("pi", 0, 1), [[1, 1]], 0, 1)
+    iota(v("pj"), [[1, 144]], 0, -1)
+    iota(v("jk"), [[0, 16], [1, 16]], 0, 0)
+    iota(v("jg"), [[1, 8], [0, 16]], 0, 0)
+    iota(v("jj"), [[1, 256]], 0, 0)
+    ms(v("rs0"), 1.0); ms(v("rb"), 0.0); ms(v("pot"), 32.0)
+    ms(v("X", 0, XO), 0.0); ms(v("X", XO + W, 2336), 0.0); ms(v("P", W, 2320), 0.0)
+    ms(v("rs0", 0, 1024, 16), 0.0); ms(v("rb", 0, 1024, 16), 512.0); ms(v("pot", 0, 256, 16), -float(1 << 24))
+    ms(cq, -0.25); ms(c0, 0.0); ms(v("cV", 0, 128), 2 * BV); ms(v("cV", 128, 256), 0.0)
+    ts(v("pi", 1, 2), v("pi", 0, 1), 15, A.bitwise_and)
+    ts(v("pi", 2, 3), v("pi", 0, 1), 4, A.arith_shift_right)
+    cp(v("col", 0, 2), v("pi", 1, 3))
+    ts(v("id32"), v("pj", 0, 128), 0.0, A.is_equal)
+    ts(v("km16"), v("jk", 0, 16), col(0), A.is_equal)
+    cp(v("r0s"), v("rdi"))
+    msg(v("r0s"), DB, v("Rl0"), "mr", 0)
+    msg(v("z0s"), DB, v("zl"), "mz", 1)
+    ms(v("XC", W, 2320), 0.0)
+    msg(v("X", XO, XO + W), -DC, v("XC", 0, W), "mx", own="sx")
+    for k in range(16):
+        act(blk("dg32", k), v("id32"), AF.Copy, scale=v("km16", k, k + 1))
+    ts(onh, v("jg"), col(1), A.is_equal)
+    cp(idb, v("id32")); cp(idh, v("id32"))
+    ts(v("tmp", 0, 128), v("jk", 0, 128), col(0), A.is_gt)
+    tt(v("tmp", 128, 256), v("tmp", 0, 128), onh, A.mult)
+    tt(M1, v("id32"), v("tmp", 128, 256), A.subtract)
+    ts(idhn, idh, -1.0, A.mult)
+    ts(v("P", 0, 1024), v("lki", 0, 1024), -1.0, A.mult, float(W), A.add)
+    ts(v("P", 1024, 2048), v("lki", 1024, 2048), -1.0, A.mult, float(W), A.add)
+    cp(v("ix"), v("Rl0"))
+    ts(R1, v("ix"), 1.0, A.add)
+
+    def consts_a():
+        for k in range(16):
+            ts(blk("dg16", k), idh, v("km16", k, k + 1), A.mult)
+
+    def consts_b():
+        ts(onn, onh, -1.0, A.mult); ts(idhalf, idb, 0.5, A.mult); ts(idn, idb, -1.0, A.mult)
+        ts(col(2), col(1), 16.0, A.mult, 15.0, A.add)
+        ts(v("oto"), v("jj", 0, 144), col(2), A.is_equal)
+        ts(v("sto"), v("pj"), 15.0, A.is_equal, v("km16", 0, 1), A.mult)
+        ts(il1, v("jj", 0, 256, 16), col(0), A.add)
+        ts(col(10), col(0), 8.0, A.is_lt, 257.0, A.mult)
+        ts(il8, il1, 8.0, A.mult)
+        ts(v("XC", W, W + 1), col(10), -1.0, A.add)
+        ms(v("sm", 0, 16), 0.0)
+        cp(v("q0"), il8)
+
+    def consts_c():
+        ts(il16, il1, 16.0, A.mult); ts(ilq, il8, -1.0, A.mult, float(W), A.add); ts(ild, il1, float(DUM), A.add)
+        ts(v("Gn", 0, 8), v("jj", 0, 8), col(1), A.is_equal)
+        ts(v("kto"), v("jj", 0, 144), col(2), A.is_equal, col(0), A.mult)
+        ts(v("Gn", 8, 16), v("Gn", 0, 8), BV, A.mult)
+        ts(v("Gn", 16, 24), v("Gn", 0, 8), 512.0, A.mult)
+        ts(col(3), col(0), 32.0, A.mult, -488.5, A.add)
+        ts(col(4), col(0), 32.0, A.mult, -494.0, A.add)
+        ts(col(5), col(0), 32.0, A.mult, -483.5, A.add)
+        ts(v("sp"), c0, 0.0, A.mult); ts(v("R1", 256, 512), c0, 0.0, A.mult)
+        ts(onB, onh, BIG, A.mult); ts(onN, onh, -BIG, A.mult); ts(idB, idh, BIG, A.mult); ts(idN, idh, -BIG, A.mult)
+        ts(id8, idb, 8.0, A.mult); ts(ido, idb, -2040.0, A.mult)
+        ts(v("ch"), c0, 256.0, A.add); cp(v("onBb"), onB)
+        ts(v("ltB"), v("jk", 0, 16), col(0), A.is_gt)
+        ms(v("D0"), -1.0)
+        for k in range(1, 16):
+            ts(blk("tri", k), onB, v("ltB", k, k + 1), A.mult)
+        cp(v("D0", 0, 256, 16), ild)
+        ts(v("OFF"), v("jk"), col(0), A.not_equal, float(1 << 21), A.mult)
+        ts(v("MB", 0, 256), v("jk"), col(0), A.is_equal, -BIG, A.mult)
+        ts(col(6), v("km16", 0, 1), 16.0, A.mult, col(0), A.add)
+        ts(col(8), v("km16", 15, 16), -16.0, A.mult, col(0), A.add)
+        ts(col(7), col(6), -1.0, A.add)
+        ts(col(9), col(8), 1.0, A.add)
+        ts(v("MB", 256, 512), v("jk"), col(7), A.is_equal, -BIG, A.mult)
+        ts(v("tmp", 0, 128), v("jk", 0, 128), col(9), A.is_equal)
+        tt(shf, v("tmp", 0, 128), onh, A.mult)
+
+    def keys(s, bank_r, bank_l, onact):
+        mms([(ps(bank_r, 0, 256), onh, v("key" + s))])
+        mms([(ps(bank_l, 256, 272), wnd("oto", k), v("key" + s, k, 256, 16)) for k in range(16)])
+        if len(onact) < 16:
+            cp(v("cr" + s), ps(bank_r, 0, 256))
+        cp(v("cl" + s, 0, 16), ps(bank_l, 256, 272))
+        if onact:
+            ts(v("cl" + s, 16, 32), ps(bank_l, 256, 272), -1.0, A.mult)
+
+    def dedupe(s, bank_r, bank_z, onact, extra):
+        lst = [(ps(bank_z, 0, 256), idb, v("OFF")), (ps(bank_z, 0, 256), onh, v("key" + s))] + extra
+        for a in range(16):
+            e = v("EE" + s, 272 * a, 272 * a + 256 - 16 * a)
+            if a in onact:
+                act(v("EA" + s, 272 * a, 272 * a + 256 - 16 * a), ps(bank_r, 16 * a, 256), AF.Abs, bias=v("cl" + s, 16 + a, 17 + a))
+                act(e, v("EA" + s, 272 * a, 272 * a + 256 - 16 * a), AF.Relu, bias=1.0, scale=-1.0)
+            else:
+                ts(e, v("cr" + s, 16 * a, 256), v("cl" + s, a, a + 1), A.is_equal)
+        for a in [a for a in range(15) if a not in onact] + [a for a in range(15) if a in onact]:
+            lst.append((ps(bank_z, 16 * a + 16, 256), v("onBb"), v("EE" + s, 272 * a + 16, 272 * a + 256 - 16 * a)))
+        lst += [(ps(bank_z, k, 256, 16), blk("tri", k), v("EE" + s, k, 272 * 15 + k + 1, 272)) for k in range(1, 16)]
+        mms(lst)
+
+    def places(bank_z, sc, out):
+        scan(v(sc), v("D0"), ps(bank_z, 0, 256), A.max, A.min)
+        ts(out, v(sc, 15, 256, 16), -1.0, A.add)
+
+    for t in range(RO):
+        last = t == RO - 1
+        z = "zl" if t == 0 else "ys%d" % (t - 1)
+        ys, yl, qu, ql, ks, kl, ns, nl, ws, wl = ["%s%d" % (k, t) for k in ("ys", "yl", "qu", "ql", "ks", "kl", "ns", "nl", "ws", "wl")]
+        Ls, hs, es = "Ls", "hs", "es"
+        oh, ohc, ohl = v(hs, 0, 256), v(hs, 256, 512), v(hs, 512, 768)
+
+        def pgather(c, tt_):
+            a, b = CH[c]
+            gather(PENG[c], v("G32" if PENG[c] == "act" else "G16", 16 * a, 16 * b), Pc, v("Rl%d" % tt_, a, b))
+            inturn("g")
+
+        def diag(c):
+            a, b = CH[c]
+            gb, dg = ("G32", "dg32") if PENG[c] == "act" else ("G16", "dg16")
+            mms([(ps(1 + c, 0, b - a), blk(dg, k), v(gb, 16 * a + k, 16 * b, 16)) for k in range(16)])
+
+        def chain1(c):
+            a, b = CH[c]
+            n, bk = b - a, 1 + c
+            ts(v("fB", a, b), ps(bk, 0, n), 0.0, A.is_equal, BIG, A.mult)
+            ts(v(Ls, a, b), ps(bk, 0, n), -1.0, A.mult, float(W), A.add)
+            mms([(ps(bk, 128, 128 + n), M1, v("fB", a, b)), (ps(bk, 128, 128 + n), idh, v("R1", a, b))])
+            mms([(ps(bk, 128 + n, 128 + 2 * n), idh, v("fB", a, b)), (ps(bk, 128 + n, 128 + 2 * n), idh, v("R1", a, b))])
+
+        def chain2(c):
+            a, b = CH[c]
+            n, bk = b - a, 1 + c
+            ts(v("uw", 2 * a, 2 * b), ps(bk, 128, 128 + 2 * n), -BIG, A.add, 0.0, A.max)
+            mms([(ps(bk, 384, 384 + n), idhn, v("fB", a, b)), (ps(bk, 384, 384 + n), onh, v("uw", 2 * a, 2 * a + n))])
+
+        def chain3(c):
+            a, b = CH[c]
+            n, bk = b - a, 1 + c
+            tt(v("ix", a, b), ps(bk, 384, 384 + n), v("uw", 2 * a + n, 2 * b), A.max)
+            ts(v("ixu", a, b), v("ix", a, b), float(XO - 1), A.add)
+
+        def xgather(c):
+            a, b = CH[c]
+            gather(XENG[c], v("xg", 16 * a, 16 * b), v("X"), v("ixu", a, b))
+            inturn("x")
+
+        def scans(c):
+            a, b = CH[c]
+            n = 16 * (b - a)
+            scan(v("smx", 16 * a, 16 * b), v("rs0", 0, n), v("xg", 16 * a, 16 * b), A.mult, A.max)
+            scan(v("smn", 16 * a, 16 * b), v("rb", 0, n), v("xg", 16 * a, 16 * b), A.add, A.min)
+
+        def ymake(a, b, bk):
+            o = ps(bk, 0, b - a)
+            mms([(o, idb, v("ct", 0, b - a)), (o, idb, v("zz", a, b)),
+                 (o, idhalf, v("smx", 16 * a + 15, 16 * b, 16)), (o, idhalf, v("smn", 16 * a + 15, 16 * b, 16))])
+            ts(v(ys, a, b), o, MAGIC, A.add, -MAGIC, A.add)
+
+        if t == 0:
+            consts_a(); consts_b(); consts_c()
+        for c in range(len(CH)):
+            pgather(c, t); diag(c); chain1(c); chain2(c); chain3(c); xgather(c); scans(c)
+            a, b = CH[c]
+            act(v("Lf", a, b), ps(1 + c, 0, b - a), AF.Identity, bias=float(W), scale=-1.0)
+        mms([(ps(6, 0, 256), onn, v("fB")), (ps(6, 0, 256), idb, v(z))])
+        act(v("zz"), ps(6, 0, 256), AF.Relu)
+        if t > 0:
+            tt(ind(XC, v("wl%d" % (t - 1))), v("nl%d" % (t - 1), 0, 256), v("nl%d" % (t - 1), 256, 512), A.add)
+        cp(v("xq"), ind(XC, v("q0") if t == 0 else v("qu%d" % (t - 1))))
+        mms([(ps(7, 256, 272), wnd("oto", k), v("xq", k, 256, 16)) for k in range(16)])
+        mms([(ps(7, 0, 256), onh, v("xq"))])
+        ts(v("sm", 32, 48), ps(7, 256, 272), 0.0, A.is_equal)
+        act(v("orow"), ps(7, 0, 256), AF.Relu, bias=1.0, scale=-1.0)
+        ts(v("sm", 48, 64), v("sm", 32, 48), -1.0, A.mult, 1.0, A.add)
+        tt(v("sm", 64, 80), v("sm", 48, 64), v("sm", 0, 16), A.mult)
+        tt(v("sm", 80, 96), v("sm", 64, 80), il8, A.add)
+        act(ps(1, 256, 512), v("Lf"), AF.Identity, bias=1.0)
+
+        for (a, b, bk) in ((0, YCUT, 5), (YCUT, 256, 6)):
+            ymake(a, b, bk)
+            a1, b1 = a // 16, b // 16
+            o = ps(bk, 256 + a1, 256 + b1)
+            mms([(o, wnd("sto", k), v(ys, a + k, b, 16)) for k in range(16)])
+            cp(v("si", a1, b1), o)
+            ts(v("si", 16 + a1, 16 + b1), v("si", a1, b1), 7, A.bitwise_and)
+            tt(v("sm", 96 + a1, 96 + b1), v("si", 16 + a1, 16 + b1), v("sm", 32 + a1, 32 + b1), A.mult)
+            tt(v("sm", 112 + a1, 112 + b1), v("sm", 96 + a1, 96 + b1), v("sm", 80 + a1, 80 + b1), A.add)
+            cp(v(qu, a1, b1), v("sm", 112 + a1, 112 + b1))
+            cp(ind(XC, v(qu, a1, b1)), v(ys, a, b))
+        msg(v(ys), DC, v(yl), "my%d" % t)
+        msg(v(qu), DC, v(ql), "mq%d" % t)
+        if last:
+            msg(v(ys), -DB, v("zol"), "mzo")
+            dma("sync", T.zo[:], ap(v("zol")), [v("zol")], [], "st")
+
+        for (a, b, e) in ECH:
+            gather(e, v("eg", 16 * a, 16 * b), XC, v(Ls, a, b))
+        if not last:
+            tt(v("sm", 0, 16), v("sm", 112, 128), il8, A.subtract)
+            ts(v("qh", 0, 16), v("sm", 112, 128), -1.0, A.mult, float(W), A.add)
+        cp(ind(Xc, v(ql)), v(yl))
+
+        def dfill(j):
+            h, kq, bk = j // 4, j % 4, 2 + j % 4
+            for kk in range(4):
+                k = 4 * kq + kk
+                o = ps(bk, 128 * kk, 128 * kk + 128)
+                mms([(o, idn, v(ys, 128 * h, 128 * h + 128)), (o, idb, v("eg", 2048 * h + k, 2048 * h + 2048, 16))])
+
+        def dread(j):
+            bk = 2 + j % 4
+            ts(v("ge", 512 * j, 512 * j + 512), ps(bk), 0.0, A.is_ge)
+            act(v("ab", 512 * j, 512 * j + 512), ps(bk), AF.Abs)
+
+        def dsum(j):
+            h, kq = j // 4, j % 4
+            if kq == 0:
+                mm(ps(6 + h, 0, 256), idb, v("cV"), True, False)
+            for kk in range(4):
+                k = 4 * kq + kk
+                mm(ps(6 + h, k, 256, 16), blk("ge", 4 * j + kk), v("Gn", 0, 16), False, False)
+            for kk in range(4):
+                k = 4 * kq + kk
+                mm(ps(6 + h, k, 128, 16), blk("ab", 4 * j + kk), v("Gn", 16, 24), False, kq == 3 and kk == 3)
+
+        def settle(h):
+            act(v("tB", 128 * h, 128 * h + 128), ps(6 + h, 128, 256), AF.Abs, bias=-7.5 * BV)
+            tt(v("km", 128 * h, 128 * h + 128), ps(6 + h, 0, 128), v("tB", 128 * h, 128 * h + 128), A.min)
+
+        for j in range(4):
+            dfill(j)
+        for j in range(8):
+            dread(j)
+            if j + 4 < 8:
+                dfill(j + 4)
+            dsum(j)
+        settle(0)
+        settle(1)
+        scan(v("S"), v("pot"), v("km"), A.add, A.max)
+        ts(v("si", 32, 48), v("S", 15, 256, 16), 1.0 - 2 * BV, A.add, 0.0, A.max)
+        ts(v("si", 48, 64), v("si", 32, 48), 511, A.bitwise_and)
+        cp(v("sp", 0, 256, 16), v("si", 48, 64))
+        scan(v("rep"), v("rs0", 0, 256), v("sp"), A.mult, A.add)
+        mms([(ps(2, 256, 512), idh, R1)])
+        mms([(ps(5, 0, 256), id8, v(ys)), (ps(5, 0, 256), ido, v("orow"))])
+        act(v("U8"), ps(5, 0, 256), AF.Abs)
+        mm(ps(0), idh, v("R1"), True, False)
+        mm(ps(0, 0, 256), idb, v("U8"), False, False)
+        mm(ps(0, 256, 512), idb, v("U8"), False, False)
+        mm(ps(0, 256, 512), v("id32"), v("Lf"), False, False)
+        if t == 1:
+            mms([(ps(3, 288, 304), shf, v("qh", 0, 16))])
+            cp(v("qh", 16, 32), ps(3, 288, 304))
+        if not last:
+            for k in range(16):
+                mms([(ps(5, k, 256, 16), blk("dg16", (k + t) % 16), v("qh", 16 * t, 16 * t + 16))])
+            act(v("Qd"), ps(5, 0, 256), AF.Copy)
+        for h in range(2):
+            mms([(ps(1, 128 * h, 128 * h + 128), v("rep", 128 * h, 128 * h + 128), idh)])
+        for j, thr in ((0, 8.5), (2, 2.5), (1, 3.0)):
+            act(v("a123", 256 * j, 256 * j + 256), ps(1, 0, 256), AF.Abs, bias=col(3 + j))
+            ts(v(hs, 256 * j, 256 * j + 256), v("a123", 256 * j, 256 * j + 256), thr, A.is_le)
+
+        tt(v("key"), ps(1, 256, 512), ohl, A.mult)
+        tt(v("key5"), ps(2, 256, 512), oh, A.mult)
+        e4, e5 = (EL4, EL5) if last else (EACT4, EACT5)
+        keys("", 3, 6, e4)
+        keys("5", 2, 7, e5)
+        ts(v("su", 32, 48), v("cl5", 0, 16), -1.0, A.add)
+        mms([(ps(1, 0, 16), wnd("kto", k), v(hs, 256 + k, 512, 16)) for k in range(16)])
+        tt(v("sm", 128, 144), ps(1, 0, 16), il16, A.add)
+        cp(v("su", 0, 16), v("sm", 128, 144))
+        gather("act", v(es), v("eg"), v("su", 0, 16))
+        mm(ps(0, 0, 256), idN, ohc, False, False)
+        mm(ps(0, 256, 512), idB, ohc, False, True)
+        act(v("v2"), ps(0, 256, 512), AF.Identity, bias=1.0 - BIG)
+        tt(v("vi"), ps(0, 0, 256), v("v2"), A.max)
+        ts(v("vj"), v("vi"), W - 1, A.bitwise_and)
+        cp(v("Rl%d" % (t + 1)), v("vj"))
+        ops[-1]["first"] = 0.0 if last else FIRST
+        if last:
+            msg(v("Rl3"), -DB, v("rol"), "mro")
+        else:
+            ts(R1, v("vj"), 1.0, A.add)
+            gather("act", v("oP"), Pc, v("su", 32, 48))
+            o = ps(6, 0, 256)
+            mms([(o, idb, v("MB", 256 * t, 256 * t + 256)), (o, idN, ohc), (o, idN, ohl), (o, v("id32"), v("oP"))])
+            act(v("bP"), o, AF.Relu)
+        dedupe("", 3, 4, e4, [(ps(4, 0, 256), onh, v("ch")), (ps(4, 0, 256), onN, ohl)])
+        places(4, "sc4", v(ks))
+        msg(v(ks), DC, v(kl), "mk%d" % t)
+        dedupe("5", 2, 5, e5, [])
+        places(5, "sc", v(ws))
+        if not last:
+            msg(v(ws), -DC, v(wl), "mw%d" % t)
+            tt(ind(v("P"), v(ws)), v("bP"), v("Qd"), A.add)
+            ops[-1]["first"] = FIRST
+            cp(ind(XC, v(ks)), c0)
+        cp(ind(Xc, v(kl)), c0)
+        gather("act", v("oX"), Xc, v("su", 32, 48))
+        o = ps(7, 0, 256)
+        mms([(o, idb, cq), (o, idhalf, v(es)), (o, onB, ohc), (o, idhalf, v("oX"))])
+        o = ps(1, 256, 512)
+        mms([(o, onN, ohc), (o, idb, v("oX"))])
+        act(v("aa"), ps(7, 0, 256), AF.Identity, bias=MAGIC - BIG)
+        ts(v(ns, 256, 512), ps(1, 256, 512), 0.0, A.max)
+        act(v(ns, 0, 256), v("aa"), AF.Relu, bias=-MAGIC)
+        tt(ind(Xc, v(ws)), v(ns, 0, 256), v(ns, 256, 512), A.add)
+        if not last:
+            msg(v(ns), -DC, v(nl), "mn%d" % t)
+
+    dma("sync", T.xo[:, 0:1024], ap(v("X", XO, XO + 1024)), [v("X")], [], "st")
+    dma("act", T.xo[:, 1024:2048], ap(v("X", XO + 1024, XO + 2048)), [v("X")], [], "st")
+    cp(v("rof"), v("rol"))
+    dma("sync", T.ro[:], ap(v("rof")), [v("rof")], [], "st")
+
+    n = len(ops)
+    succ = [[] for _ in range(n)]
+    left = [0] * n
+    for k, o in enumerate(ops):
+        pre = set(o["deps"]) | set(o["order"])
+        left[k] = len(pre)
+        for j in pre:
+            succ[j].append(k)
+    prio = [0.0] * n
+    for k in range(n - 1, -1, -1):
+        o = ops[k]
+        prio[k] = o["cost"] + o.get("first", 0.0) + max([0.0] + [prio[j] + (o["lat"] + HOP if k in ops[j]["deps"] else 0.0) for j in succ[k]])
+    est = [0.0] * n
+    free = {}
+    ready = [k for k in range(n) if left[k] == 0]
+    seq = []
+    while ready:
+        def start(k):
+            return max(est[k], free.get(ops[k]["q"], 0.0))
+        k0 = min(ready, key=lambda k: (start(k), -prio[k]))
+        lim = start(k0) + WIN * ops[k0]["cost"]
+        k = max([j for j in ready if ops[j]["q"] == ops[k0]["q"] and start(j) <= lim], key=lambda j: (prio[j], -j))
+        ready.remove(k)
+        seq.append(k)
+        o = ops[k]
+        end = start(k) + o["cost"]
+        free[o["q"]] = end if o["q"] != "land" else 0.0
+        for j in succ[k]:
+            est[j] = max(est[j], end + (o["lat"] + HOP if k in ops[j]["deps"] else 0.0))
+            left[j] -= 1
+            if left[j] == 0:
+                ready.append(j)
+    pos = {k: i for i, k in enumerate(seq)}
+    need = set()
+    for o in ops:
+        best = {}
+        for j in o["deps"]:
+            if ops[j]["tok"] is None and pos[j] > pos.get(best.get(ops[j]["q"]), -1):
+                best[ops[j]["q"]] = j
+        o["deps"] = [j for j in sorted(o["deps"]) if ops[j]["tok"] is not None] + sorted(best.values())
+        need.update(best.values())
+    eng = {"dve": g.vector, "act": g.scalar, "pe": g.tensor, "pool": g, "sync": g.sync}
+    seen = {q: {} for q in eng}
+    toks = {}
+    for k in seq:
+        o = ops[k]
+        q = o["q"]
+        if o["tok"] is not None:
+            toks[k] = o["tok"]
+        if q == "land":
+            continue
+        for j in o["deps"]:
+            sem, val = toks[j]
+            if seen[q].get(sem, 0) < val:
+                eng[q].wait_ge(T.sem[sem], val)
+                seen[q][sem] = val
+        r = o["fn"]()
+        if k in need:
+            total[q] = total.get(q, 0) + 1
+            r.then_inc(T.sem[q], 1)
+            toks[k] = (q, total[q])
+    for sem in SEMAPHORES:
+        if total.get(sem, 0) and max(seen[q].get(sem, 0) for q in seen) < total[sem]:
+            g.wait_ge(T.sem[sem], total[sem])

@@ -1,44 +1,47 @@
 from concourse.mybir import AluOpType, ActivationFunctionType
 
 N, W, E, RO, DB, DC = 8, 2048, 256, 3, 3, 2
-XO = 16
-DUM = 2064
-BIG = 4096.0
+PAD = 80
+TW = PAD + W
+BIG, BIG8 = 4096.0, 8192.0
 BV = float(1 << 22)
 MAGIC = 12582912.0
-CH = [(0, 64), (64, 128), (128, 192), (192, 256)]
-PENG = ["dve", "act", "act", "act"]
-XENG = ["act"] * 5
-YCUT = 192
-ECH = [(0, 64, "dve"), (64, 128, "act"), (128, 192, "dve"), (192, 256, "act")]
-EACT4 = []
-EACT5 = []
-EL4, EL5 = [], []
-FIRST = 3000.0
-CYC, GAT, SCA, PEC, FIX, HOP, FAR, BW, WIN = 1.04, 1.56, 3.8, 0.53, 30.0, 60.0, 2000.0, 60.0, 0.25
+EOFF, YOFF = -127.5, -127.5625
+PG0 = [(128, 192, "dve"), (192, 256, "act"), (0, 48, "dve"), (48, 128, "act")]
+PG = [(128, 192, "dve"), (192, 256, "act"), (0, 64, "act"), (64, 128, "act")]
+XG0 = [(192, 256, "act"), (128, 192, "act"), (96, 128, "dve"), (32, 96, "act"), (0, 32, "act")]
+XG = [(192, 256, "act"), (128, 192, "act"), (64, 128, "act"), (32, 64, "act"), (0, 32, "act")]
+YC = [(64, 256), (0, 64)]
+EG = [(128, 160, "dve"), (160, 192, "act"), (192, 224, "act"), (224, 256, "act"), (0, 32, "act"), (32, 64, "act"), (64, 96, "act"), (96, 128, "act")]
+ENG = {"u2": "dve", "u1": "dve", "K": ["act"] * 4, "cT": ["act"] * 4, "xq": "act", "RU": "act", "cap": "act", "oP": "act", "oX": ("dve", "act")}
+CYC, GAT, SCA, PEC, FIX, FIXA, FIXP, HOP, FAR, BW = 1.04, 1.56, 3.8, 0.525, 30.0, 60.0, 5.0, 60.0, 3000.0, 60.0
+START = 4000.0
+SPAN = []
+TAG = [""]
+SEG = [16 * r * (r + 1) for r in range(4)]
+ORDER = []
+SWEEPS = 3
+SHAKES = 1200
 
 F, H, B, I, U = "float32", "float16", "bfloat16", "int32", "uint16"
 BUFS = [
-    ("X", 2336, B), ("P", 2320, F), ("lki", 2048, I), ("rdi", 256, I), ("r0s", 256, U), ("z0s", 256, B), ("zl", 256, B),
-    ("R1", 512, H), ("G32", 4096, F), ("G16", 4096, H), ("fB", 256, H), ("uw", 512, H),
-    ("ix", 256, F), ("ixu", 256, U), ("xg", 4096, B), ("smx", 4096, B), ("smn", 4096, B), ("zz", 256, B), ("Lf", 256, F),
-    ("xq", 256, H), ("sm", 192, F), ("si", 64, I), ("su", 64, U), ("qh", 32, H), ("eg", 4096, B), ("ge", 4096, B), ("ab", 4096, B),
-    ("tB", 256, F), ("km", 256, F), ("S", 256, F), ("sp", 256, H), ("rep", 256, H), ("a123", 768, B),
-    ("key", 256, H), ("cr", 256, H), ("EE", 16 * 272, B), ("sc", 256, F), ("sc4", 256, F), ("U8", 256, B), ("Qd", 256, F),
-    ("oP", 256, F), ("oX", 256, B), ("bP", 256, F), ("aa", 256, F), ("v2", 256, F), ("vi", 256, I), ("vj", 256, I),
-    ("rol", 256, U), ("rof", 256, F), ("zol", 256, B), ("Rl3", 256, U),
-    ("pj", 144, F), ("jg", 128, F), ("jk", 256, F), ("jj", 256, F), ("pi", 8, I), ("col", 16, F), ("km16", 16, F), ("ltB", 16, F),
-    ("id32", 128, F), ("idb", 128 * 5, B), ("idh", 128 * 5, H), ("onh", 128 * 5, H),
-    ("dg32", 2048, F), ("dg16", 2048, H), ("tri", 2048, B), ("oto", 144, H), ("kto", 144, H), ("sto", 144, B),
-    ("D0", 256, F), ("OFF", 256, B), ("MB", 512, B), ("rs0", 1024, B), ("rb", 1024, B), ("pot", 256, B), ("il", 80, F), ("q0", 16, U),
-    ("Gn", 32, B), ("cV", 256, B), ("ct", 512, B), ("ch", 256, H), ("tmp", 256, F),
+    ("XX", 2 * TW + 16, B), ("P", TW, I), ("rdi", 256, I), ("r0s", 256, U), ("z0s", 256, B), ("zl", 256, B),
+    ("R1", 256, H), ("G16", 4096, H), ("u2", 256, H), ("u1", 256, H), ("ix", 256, H), ("ixu", 256, U), ("Ls", 256, U), ("L1", 256, H),
+    ("xg", 4096, B), ("smx", 4096, B), ("smn", 4096, B), ("zz", 256, B), ("xq", 256, H), ("orow", 256, B), ("D0", 256, F),
+    ("sq", 256, F), ("si", 64, I), ("qf", 16, F), ("qh", 16, H), ("yp", 256, H), ("yT", 256, H), ("U8", 256, B), ("cap", 256, H),
+    ("eg", 4096, B), ("Mx", 4096, H), ("Pr", 512, H), ("tB", 256, F), ("km", 256, F), ("S", 256, F), ("sp", 256, H), ("rep", 256, H),
+    ("st", 1024, H), ("KK", 512, H), ("D32", 256, F), ("RU", 256, F), ("vi", 256, I), ("vj", 256, I), ("cT", 768, H), ("cT3", 256, F), ("tl", 32, U),
+    ("AD", 1280, F), ("sc", 1280, F), ("ends", 2, U), ("oP", 256, H), ("nP", 256, F), ("oX", 512, B), ("Rf", 256, F), ("rol", 256, F), ("zol", 256, B),
+    ("pj", 144, F), ("jg", 128, F), ("jk", 256, F), ("ramp", 256, B), ("pi", 8, I), ("col", 16, F), ("km16", 16, F),
+    ("id32", 128, F), ("idb", 128 * 5, B), ("idh", 128 * 8, H), ("onh", 128 * 3, H), ("one", 512, H),
+    ("dg", 2080, H), ("EX", 2048, H), ("oto", 144, H), ("c256", 16, H), ("OFF", 256, B), ("MB", 144, B), ("rs0", 1024, B), ("rb", 1024, B),
+    ("pot", 128, B), ("il8", 16, F), ("q0", 16, U), ("Gn", 8, H), ("Gn32", 8, F), ("GM", 32, H), ("GE", 8, B), ("YS", 512, H),
+    ("cV", 128, B), ("cq", 256, B), ("c0", 64, B), ("SEL", 320, H), ("RS", 320, B), ("tmp", 512, F),
 ]
 for _t in range(RO):
     BUFS += [("%s%d" % (_n, _t), _c, _d) for _n, _c, _d in [
-        ("Rl", 256, U), ("ys", 256, B), ("yl", 256, B), ("qu", 16, U), ("ql", 16, U), ("ks", 16, U), ("kl", 16, U),
-        ("ns", 512, B), ("nl", 512, B), ("ws", 16, U), ("wl", 16, U)]]
-BUFS += [("XC", 2320, B), ("Ls", 256, U), ("orow", 256, B), ("hs", 768, H), ("es", 256, B), ("key5", 256, H), ("cr5", 256, H),
-         ("EE5", 16 * 272, B), ("EA", 16 * 272, B), ("EA5", 16 * 272, B), ("cl", 32, F), ("cl5", 32, F), ("onBb", 128, B), ("L1", 256, F)]
+        ("Rl", 256, U), ("ys", 256, B), ("yl", 256, B), ("qu", 16, U), ("ql", 16, U), ("ks", 32, U), ("kl", 32, U),
+        ("ns", 256, B), ("nl", 256, B), ("ws", 32, U), ("wl", 32, U)]]
 SCRATCH = {}
 PLACE = {}
 for _n, _c, _d in BUFS:
@@ -55,7 +58,7 @@ for _t in range(8):
     PLACE["ps%d" % _t] = ("ps%d" % _t, 0, 512)
 
 SEMAPHORES = ["dve", "act", "pe", "pool", "sent", "st", "ld0", "ld1", "ld2", "ld3", "ld4", "mr", "mz", "mro", "mzo", "mx", "sx"] + \
-    ["m%s%d" % (k, t) for t in range(RO) for k in ("y", "q", "k", "n", "w")]
+    ["m%s%d" % (k, t) for t in range(RO) for k in ("y", "q", "k", "j", "n", "w")]
 
 
 def rank_program(g, core, T, topo):
@@ -67,9 +70,9 @@ def rank_program(g, core, T, topo):
     ops = []
     acc = {}
 
-    def v(name, a=0, b=None, s=1):
-        p, o, n = PLACE[name]
-        return (p, o + a, o + (n if b is None else b), s, name)
+    def v(name, a=0, b=None, s=1, n=128, p0=0):
+        p, o, c = PLACE[name]
+        return (p, o + a, o + (c if b is None else b), s, name, n, p0)
 
     def ind(win, off):
         return ("*", win, off)
@@ -77,12 +80,13 @@ def rank_program(g, core, T, topo):
     def ap(x):
         if x[0] == "*":
             return ap(x[1]).indirect(ap(x[2]))
-        return T[x[0]][:, x[1]:x[2]] if x[3] == 1 else T[x[0]][:, x[1]:x[2]:x[3]]
+        rows = slice(None) if x[5] == 128 else slice(x[6], x[6] + x[5])
+        return T[x[0]][rows, x[1]:x[2]] if x[3] == 1 else T[x[0]][rows, x[1]:x[2]:x[3]]
 
     def arg(x):
         return ap(x) if isinstance(x, tuple) else x
 
-    def rec(q, fn, reads, writes, tok=None, kind=None):
+    def rec(q, fn, reads, writes, tok=None, kind=None, chain=None):
         k = len(ops)
         deps, order = set(), set()
         rs, ws = [], []
@@ -93,14 +97,15 @@ def rank_program(g, core, T, topo):
             x = reads[0] if reads else (o if o else None)
             size = 128 * (x[2] - x[1]) * (4 if SCRATCH[x[0]][2] in (F, I) else 2)
             if q == "land":
-                cost, lat = 0.0, FAR + size / BW
+                cost, lat = 0.0, FAR + size / BW + (START if TAG[0] == "init" else 0.0)
                 order.add(k - 1)
             elif q == "pool":
                 cost, lat = 400.0, FAR + size / BW
             else:
                 cost, lat = (size / 250.0, 1800.0) if q == "sync" else (60.0, 1800.0 + size / 250.0)
         elif q == "pe":
-            cost = max(64, len(range(o[1], o[2], o[3]))) * PEC * (4 if SCRATCH[reads[0][0]][2] == F else 1)
+            m = len(range(reads[0][1], reads[0][2], reads[0][3]))
+            cost = FIXP + max(min(64, m), len(range(o[1], o[2], o[3]))) * PEC * (4 if SCRATCH[reads[0][0]][2] == F else 1)
         elif o[0] == "*":
             cost = 55 + 16 * (o[2][2] - o[2][1]) * SCA * CYC
         else:
@@ -113,7 +118,7 @@ def rank_program(g, core, T, topo):
                     per = 1.0 if any(SCRATCH[x[0]][0] == "psum" for x in full) else 2.0
                 elif q == "dve" and all(SCRATCH[x[0]][2] in (H, B, U) for x in full + [o]):
                     per = 0.5
-                cost = FIX + max(64, n * per) * CYC + (100 if q == "pool" else 0)
+                cost = (FIXA if q == "act" else FIX) + max(64, n * per) * CYC + (100 if q == "pool" else 0)
         for x in reads:
             if isinstance(x, tuple):
                 rs += [x[1], x[2]] if x[0] == "*" else [x]
@@ -137,23 +142,24 @@ def rank_program(g, core, T, topo):
                     ep[1].append((x[1], x[2], k, wr))
                     continue
                 rd_, wr_ = acc.setdefault(x[4], ([], []))
-                deps.update(a[2] for a in (rd_ + wr_ if wr else wr_) if a[0] < x[2] and x[1] < a[1] and a[2] != k)
+                deps.update(a[2] for a in (rd_ + wr_ if wr else wr_)
+                            if a[0] < x[2] and x[1] < a[1] and a[3] < x[6] + x[5] and x[6] < a[4] and a[2] != k)
                 if wr and x[3] == 1:
-                    rd_[:] = [a for a in rd_ if not (x[1] <= a[0] and a[1] <= x[2])]
-                    wr_[:] = [a for a in wr_ if not (x[1] <= a[0] and a[1] <= x[2])]
-                (wr_ if wr else rd_).append((x[1], x[2], k))
+                    for z in (rd_, wr_):
+                        z[:] = [a for a in z if not (x[1] <= a[0] and a[1] <= x[2] and x[6] <= a[3] and a[4] <= x[6] + x[5])]
+                (wr_ if wr else rd_).append((x[1], x[2], k, x[6], x[6] + x[5]))
         if q == "sync":
             order.update(acc.get("*sync", []))
             acc["*sync"] = [k]
-        ops.append({"q": q, "fn": fn, "deps": deps, "tok": tok, "order": order, "cost": cost, "lat": lat})
+        ops.append({"q": q, "fn": fn, "deps": deps, "tok": tok, "order": order, "cost": cost, "lat": lat, "chain": chain, "tag": TAG[0]})
 
     def inturn(name):
         name = "*" + name + ops[-1]["q"]
         ops[-1]["order"].update(acc.get(name, []))
         acc[name] = [len(ops) - 1]
 
-    def cp(out, in_):
-        rec("dve", lambda: g.vector.tensor_copy(ap(out), ap(in_)), [in_], [out])
+    def cp(out, in_, chain=None):
+        rec("dve", lambda: g.vector.tensor_copy(ap(out), ap(in_)), [in_], [out], chain=chain)
 
     def tt(out, a, b, op):
         rec("dve", lambda: g.vector.tensor_tensor(ap(out), ap(a), ap(b), op), [a, b], [out], kind="tt")
@@ -176,9 +182,9 @@ def rank_program(g, core, T, topo):
     def mm(o, l, r, start, stop):
         rec("pe", lambda: g.tensor.matmul(ap(o), ap(l), ap(r), start, stop), [l, r], [o])
 
-    def mms(lst):
+    def mms(lst, start=True, stop=True):
         for i, (o, l, r) in enumerate(lst):
-            mm(o, l, r, i == 0, i == len(lst) - 1)
+            mm(o, l, r, start and i == 0, stop and i == len(lst) - 1)
 
     def iota(out, pat, base, cm):
         if SCRATCH[out[0]][2] == I:
@@ -186,11 +192,30 @@ def rank_program(g, core, T, topo):
         else:
             rec("pool", lambda: g.iota(ap(out), pat, base, cm, allow_small_or_imprecise_dtypes=True), [], [out])
 
-    def gather(eng, out, win, off):
+    def lin(eng, out, in_, bias=0.0, scale=1.0):
         if eng == "act":
+            act(out, in_, AF.Identity, bias=bias, scale=scale)
+        else:
+            ts(out, in_, scale, A.mult, bias, A.add)
+
+    def relu(eng, out, in_, bias=0.0):
+        if eng == "act":
+            act(out, in_, AF.Relu, bias=bias)
+        else:
+            ts(out, in_, bias, A.add, 0.0, A.max)
+
+    def gather(eng, out, win, off, bias=None):
+        if bias is not None:
+            lin(eng, out, ind(win, off), bias)
+        elif eng == "act":
             act(out, ind(win, off), AF.Copy)
         else:
             cp(out, ind(win, off))
+
+    def scatter(win, lst, src, blocks, chain):
+        for b in blocks:
+            a = 16 * (b // 2) + 4 * (b % 2)
+            cp(ind(win, v(lst, a, a + 4)), v("c0") if src is None else blk(src, b, 64), chain=chain)
 
     total = {}
 
@@ -214,347 +239,299 @@ def rank_program(g, core, T, topo):
             tok=(own, None if own == "sent" else total[own]))
         rec("land", None, [], [dst], tok=(sem, total[sem]))
 
-    def ps(b, a=0, e=512, s=1):
-        return v("ps%d" % b, a, e, s)
+    def ps(b, a=0, e=512, s=1, n=128):
+        return v("ps%d" % b, a, e, s, n)
 
     def col(j):
         return v("col", j, j + 1)
 
-    def blk(name, k):
-        return v(name, 128 * k, 128 * k + 128)
+    def blk(name, k, w=128):
+        return v(name, w * k, w * k + w)
 
-    def wnd(name, k):
-        return v(name, 15 - k, 143 - k)
+    Xw, XCw, XX, Pw = v("XX", 0, TW), v("XX", TW, 2 * TW + 16), v("XX"), v("P")
+    idb, idhalf, id8, ido, s0h = [blk("idb", j) for j in range(5)]
+    idh, idhn, idN4, idB8, idN8, idn16, id1008, M1 = [blk("idh", j) for j in range(8)]
+    onh, onB, onN = [blk("onh", j) for j in range(3)]
+    id32, cq = v("id32"), v("cq")
+    DOWN = [3, 2, 1, 0]
 
-    Xc = v("X", XO, 2336)
-    XC = v("XC")
-    Pc = v("P", 0, W)
-    R1 = v("R1", 0, 256)
-    idb, idhalf, idn, id8, ido = [blk("idb", j) for j in range(5)]
-    idh, idhn, idB, idN, M1 = [blk("idh", j) for j in range(5)]
-    onh, onB, onN, shf, onn = [blk("onh", j) for j in range(5)]
-    cq, c0 = v("ct", 0, 256), v("ct", 256, 512)
-    il1, il8, il16, ilq, ild = [v("il", 16 * j, 16 * j + 16) for j in range(5)]
+    def dg(k, shift=0):
+        a = 16 + 128 * k - (shift if k + shift < 16 else shift - 16)
+        return v("dg", a, a + 128)
 
+    TAG[0] = "init"
     dma("sync", ap(v("rdi")), T.rd[:], [], [v("rdi")], "ld0")
     dma("act", ap(v("z0s")), T.z0[:], [], [v("z0s")], "ld1")
-    dma("sync", ap(v("lki", 0, 1024)), T.lk[:, 0:1024], [], [v("lki", 0, 1024)], "ld2")
-    dma("sync", ap(v("lki", 1024, 2048)), T.lk[:, 1024:2048], [], [v("lki", 1024, 2048)], "ld3")
-    dma("sync", ap(v("X", XO, XO + W)), T.x0[:], [], [v("X", XO, XO + W)], "ld4")
+    dma("sync", ap(v("XX", PAD, TW)), T.x0[:], [], [v("XX", PAD, TW)], "ld4")
+    for j in range(2):
+        o = v("P", PAD + 1024 * j, PAD + 1024 * j + 1024)
+        dma("sync", ap(o), T.lk[:, 1024 * j:1024 * j + 1024], [], [o], "ld%d" % (2 + j))
     iota(v("pi", 0, 1), [[1, 1]], 0, 1)
     iota(v("pj"), [[1, 144]], 0, -1)
     iota(v("jk"), [[0, 16], [1, 16]], 0, 0)
     iota(v("jg"), [[1, 8], [0, 16]], 0, 0)
-    iota(v("jj"), [[1, 256]], 0, 0)
-    ms(v("rs0"), 1.0); ms(v("rb"), 0.0); ms(v("pot"), 32.0)
-    ms(v("X", 0, XO), 0.0); ms(v("X", XO + W, 2336), 0.0); ms(v("P", W, 2320), 0.0)
-    ms(v("rs0", 0, 1024, 16), 0.0); ms(v("rb", 0, 1024, 16), 512.0); ms(v("pot", 0, 256, 16), -float(1 << 24))
-    ms(cq, -0.25); ms(c0, 0.0); ms(v("cV", 0, 128), 2 * BV); ms(v("cV", 128, 256), 0.0)
+    ts(v("r0s"), v("rdi"), float(PAD), A.add)
+    msg(v("r0s"), DB, v("Rl0"), "mr", 0)
+    msg(v("z0s"), DB, v("zl"), "mz", 1)
+    ops[-2]["order"].add(len(ops) - 4)
+    ms(v("XX", 0, PAD), 0.0); ms(v("XX", TW, TW + PAD), 0.0); ms(v("XX", 2 * TW, 2 * TW + 16), 0.0); ms(v("P", 0, PAD), 0)
+    msg(v("XX", PAD, TW), -DC, v("XX", TW + PAD, 2 * TW), "mx", own="sx")
+    ops[-2]["order"].add(len(ops) - 8)
+    ts(v("R1"), v("Rl0"), 1.0 - PAD, A.add)
+
     ts(v("pi", 1, 2), v("pi", 0, 1), 15, A.bitwise_and)
     ts(v("pi", 2, 3), v("pi", 0, 1), 4, A.arith_shift_right)
     cp(v("col", 0, 2), v("pi", 1, 3))
-    ts(v("id32"), v("pj", 0, 128), 0.0, A.is_equal)
-    ts(v("km16"), v("jk", 0, 16), col(0), A.is_equal)
-    cp(v("r0s"), v("rdi"))
-    msg(v("r0s"), DB, v("Rl0"), "mr", 0)
-    msg(v("z0s"), DB, v("zl"), "mz", 1)
-    ms(v("XC", W, 2320), 0.0)
-    msg(v("X", XO, XO + W), -DC, v("XC", 0, W), "mx", own="sx")
+    ts(id32, v("pj", 0, 128), 0.0, A.is_equal)
+    ts(v("km16"), v("jk", 0, 16), col(0), A.is_equal, BIG, A.mult)
+    ms(cq, -0.25); ms(v("c0"), 0.0)
+    for o, c in ((blk("one", 0, 256), -4.0), (blk("one", 1, 256), -4.0), (v("sp"), -128.0), (v("D0"), 4.0)):
+        lin("act", o, cq, 0.0, c)
+    ts(v("dg", 0, 16), v("cq", 0, 16), 0.0, A.mult); ts(v("dg", 2064, 2080), v("cq", 0, 16), 0.0, A.mult)
     for k in range(16):
-        act(blk("dg32", k), v("id32"), AF.Copy, scale=v("km16", k, k + 1))
+        act(dg(k), id32, AF.Copy, scale=v("km16", k, k + 1))
+    cp(idh, id32); cp(idb, id32)
+    for o, c in ((idhn, -1.0), (idN4, -BIG), (idB8, BIG8), (idN8, -BIG8), (idn16, -16.0), (id1008, 1008.0)):
+        ts(o, idh, c, A.mult)
+    for o, c in ((idhalf, 0.5), (id8, 8.0), (ido, -2040.0)):
+        ts(o, idb, c, A.mult)
     ts(onh, v("jg"), col(1), A.is_equal)
-    cp(idb, v("id32")); cp(idh, v("id32"))
+    ts(onB, onh, BIG, A.mult); ts(onN, onh, -BIG, A.mult)
     ts(v("tmp", 0, 128), v("jk", 0, 128), col(0), A.is_gt)
-    tt(v("tmp", 128, 256), v("tmp", 0, 128), onh, A.mult)
-    tt(M1, v("id32"), v("tmp", 128, 256), A.subtract)
-    ts(idhn, idh, -1.0, A.mult)
-    ts(v("P", 0, 1024), v("lki", 0, 1024), -1.0, A.mult, float(W), A.add)
-    ts(v("P", 1024, 2048), v("lki", 1024, 2048), -1.0, A.mult, float(W), A.add)
-    cp(v("ix"), v("Rl0"))
-    ts(R1, v("ix"), 1.0, A.add)
-
-    def consts_a():
-        for k in range(16):
-            ts(blk("dg16", k), idh, v("km16", k, k + 1), A.mult)
-
-    def consts_b():
-        ts(onn, onh, -1.0, A.mult); ts(idhalf, idb, 0.5, A.mult); ts(idn, idb, -1.0, A.mult)
-        ts(col(2), col(1), 16.0, A.mult, 15.0, A.add)
-        ts(v("oto"), v("jj", 0, 144), col(2), A.is_equal)
-        ts(v("sto"), v("pj"), 15.0, A.is_equal, v("km16", 0, 1), A.mult)
-        ts(il1, v("jj", 0, 256, 16), col(0), A.add)
-        ts(col(10), col(0), 8.0, A.is_lt, 257.0, A.mult)
-        ts(il8, il1, 8.0, A.mult)
-        ts(v("XC", W, W + 1), col(10), -1.0, A.add)
-        ms(v("sm", 0, 16), 0.0)
-        cp(v("q0"), il8)
-
-    def consts_c():
-        ts(il16, il1, 16.0, A.mult); ts(ilq, il8, -1.0, A.mult, float(W), A.add); ts(ild, il1, float(DUM), A.add)
-        ts(v("Gn", 0, 8), v("jj", 0, 8), col(1), A.is_equal)
-        ts(v("kto"), v("jj", 0, 144), col(2), A.is_equal, col(0), A.mult)
-        ts(v("Gn", 8, 16), v("Gn", 0, 8), BV, A.mult)
-        ts(v("Gn", 16, 24), v("Gn", 0, 8), 512.0, A.mult)
-        ts(col(3), col(0), 32.0, A.mult, -488.5, A.add)
-        ts(col(4), col(0), 32.0, A.mult, -494.0, A.add)
-        ts(col(5), col(0), 32.0, A.mult, -483.5, A.add)
-        ts(v("sp"), c0, 0.0, A.mult); ts(v("R1", 256, 512), c0, 0.0, A.mult)
-        ts(onB, onh, BIG, A.mult); ts(onN, onh, -BIG, A.mult); ts(idB, idh, BIG, A.mult); ts(idN, idh, -BIG, A.mult)
-        ts(id8, idb, 8.0, A.mult); ts(ido, idb, -2040.0, A.mult)
-        ts(v("ch"), c0, 256.0, A.add); cp(v("onBb"), onB)
-        ts(v("ltB"), v("jk", 0, 16), col(0), A.is_gt)
-        ms(v("D0"), -1.0)
-        for k in range(1, 16):
-            ts(blk("tri", k), onB, v("ltB", k, k + 1), A.mult)
-        cp(v("D0", 0, 256, 16), ild)
-        ts(v("OFF"), v("jk"), col(0), A.not_equal, float(1 << 21), A.mult)
-        ts(v("MB", 0, 256), v("jk"), col(0), A.is_equal, -BIG, A.mult)
-        ts(col(6), v("km16", 0, 1), 16.0, A.mult, col(0), A.add)
-        ts(col(8), v("km16", 15, 16), -16.0, A.mult, col(0), A.add)
-        ts(col(7), col(6), -1.0, A.add)
-        ts(col(9), col(8), 1.0, A.add)
-        ts(v("MB", 256, 512), v("jk"), col(7), A.is_equal, -BIG, A.mult)
-        ts(v("tmp", 0, 128), v("jk", 0, 128), col(9), A.is_equal)
-        tt(shf, v("tmp", 0, 128), onh, A.mult)
-
-    def keys(s, bank_r, bank_l, onact):
-        mms([(ps(bank_r, 0, 256), onh, v("key" + s))])
-        mms([(ps(bank_l, 256, 272), wnd("oto", k), v("key" + s, k, 256, 16)) for k in range(16)])
-        if len(onact) < 16:
-            cp(v("cr" + s), ps(bank_r, 0, 256))
-        cp(v("cl" + s, 0, 16), ps(bank_l, 256, 272))
-        if onact:
-            ts(v("cl" + s, 16, 32), ps(bank_l, 256, 272), -1.0, A.mult)
-
-    def dedupe(s, bank_r, bank_z, onact, extra):
-        lst = [(ps(bank_z, 0, 256), idb, v("OFF")), (ps(bank_z, 0, 256), onh, v("key" + s))] + extra
-        for a in range(16):
-            e = v("EE" + s, 272 * a, 272 * a + 256 - 16 * a)
-            if a in onact:
-                act(v("EA" + s, 272 * a, 272 * a + 256 - 16 * a), ps(bank_r, 16 * a, 256), AF.Abs, bias=v("cl" + s, 16 + a, 17 + a))
-                act(e, v("EA" + s, 272 * a, 272 * a + 256 - 16 * a), AF.Relu, bias=1.0, scale=-1.0)
-            else:
-                ts(e, v("cr" + s, 16 * a, 256), v("cl" + s, a, a + 1), A.is_equal)
-        for a in [a for a in range(15) if a not in onact] + [a for a in range(15) if a in onact]:
-            lst.append((ps(bank_z, 16 * a + 16, 256), v("onBb"), v("EE" + s, 272 * a + 16, 272 * a + 256 - 16 * a)))
-        lst += [(ps(bank_z, k, 256, 16), blk("tri", k), v("EE" + s, k, 272 * 15 + k + 1, 272)) for k in range(1, 16)]
-        mms(lst)
-
-    def places(bank_z, sc, out):
-        scan(v(sc), v("D0"), ps(bank_z, 0, 256), A.max, A.min)
-        ts(out, v(sc, 15, 256, 16), -1.0, A.add)
+    tt(v("tmp", 128, 256), v("tmp", 0, 128), onN, A.mult)
+    tt(M1, id32, v("tmp", 128, 256), A.add)
+    ts(col(2), v("km16", 0, 1), 0.5 / BIG, A.mult)
+    ts(s0h, onh, col(2), A.mult)
+    iota(v("rs0"), [[0, 64], [256, 16]], 0, 0)
+    lin("act", v("rb"), v("rs0"), 256.0, -1.0)
+    for j in range(4):
+        e = blk("EX", j, 512)
+        rec("pool", lambda e=e, j=j: g.affine_select(ap(e), ap(v("one")), [[1, 32], [0, 16]], A.is_equal, 0.0, 32 * j, -1), [v("one")], [e])
+    ts(col(3), col(0), -1.0, A.mult, 15.0, A.add)
+    ts(v("oto"), v("pj"), col(3), A.is_equal, -256.0, A.mult)
+    iota(v("ramp"), [[512, 16], [0, 16]], 0, 0)
+    ramp = v("ramp", 0, 256, 16)
+    ts(v("c256"), ramp, 256.0, A.add)
+    ts(v("OFF"), v("jk"), col(0), A.not_equal, float(1 << 21), A.mult)
+    ts(v("MB"), v("jk", 0, 144), col(0), A.is_equal, BIG8, A.mult)
+    ms(v("pot"), 32.0); ms(v("pot", 0, 128, 16), -float(1 << 24))
+    ts(v("si", 16, 32), ramp, 0.0, A.add)
+    ts(col(9), col(0), 8.0, A.mult, float(PAD), A.add)
+    ts(v("q0"), ramp, 0.25, A.mult, col(9), A.add)
+    ts(v("il8"), ramp, -0.75, A.mult, col(9), A.add)
+    ts(v("Gn32"), v("jg", 0, 128, 16), col(1), A.is_equal)
+    cp(v("Gn"), v("Gn32"))
+    ts(col(4), col(0), 8.0, A.is_lt); ts(col(5), col(0), 8.0, A.is_ge)
+    ts(v("XX", 2 * TW, 2 * TW + 1), col(4), 256.0, A.mult, -1.0, A.add)
+    for j, c in enumerate((col(4), col(5), 16.0, 16.0)):
+        ts(blk("GM", j, 8), v("Gn32"), c, A.mult)
+    ts(v("GE"), v("Gn32"), -512.0, A.mult)
+    for j, (c, d) in enumerate(((col(4), -1.0), (col(5), -1.0), (-16.0, 1.0), (496.0, 1.0))):
+        ts(blk("YS", j), onh, c, A.mult, d, A.mult)
+    ms(v("cV"), 2 * BV)
+    ms(v("RS"), 0.0)
+    for r in range(4):
+        a, n = SEG[r], 16 * (r + 1)
+        iota(v("AD", a, a + 2 * n), [[4, 2], [0, n]], r, -1)
+        iota(v("sc", a, a + 2 * n), [[0, 2], [1, n]], -16 * r, 0)
+        ms(v("sc", 320 + a, 320 + a + 2 * n), 16.0 * r)
+        ms(v("RS", a, a + 2 * n, n), float(1 << 25))
+    ts(v("SEL"), v("AD", 0, 320), 0.0, A.is_equal, -BIG, A.mult)
+    ts(v("sc", 640, 960), v("sc", 0, 320), col(0), A.is_ge, BIG, A.mult)
+    ts(v("sc", 960, 1280), v("sc", 320, 640), col(0), A.add, 1.0 / BIG, A.mult)
+    tt(v("SEL", 0, 320, 1, 16, 32), v("sc", 640, 960, 1, 16, 32), v("sc", 960, 1280, 1, 16, 32), A.add)
+    for j in range(3):
+        ts(blk("cT", j, 256), cq, 0.0, A.mult)
+        ts(v("cT", 256 * j, 256 * j + 256, 1, 16, 32), v("jk", 0, 256, 1, 16, 32), v("col", 0, 1, 1, 16, 32), A.is_equal, BIG, A.mult)
+    for r in range(4):
+        a, n = SEG[r], 16 * (r + 1)
+        e = v("SEL", a + n - 1, a + 2 * n, n, 8)
+        ts(e, e, -1.0 / BIG, A.mult)
+        e = v("SEL", a + n - 1, a + 2 * n, n, 16, 32)
+        ts(e, e, 0.0, A.mult, (PAD - 1.0) / BIG, A.add)
+    ts(v("pi", 3, 4), v("pi", 0, 1), 3, A.bitwise_and)
+    ts(v("pi", 4, 5), v("pi", 0, 1), 2, A.arith_shift_right, 1, A.bitwise_and)
+    ts(col(6), v("pi", 3, 4), 1.0, A.add, 16.0, A.mult)
+    tt(col(7), v("pi", 3, 4), v("pi", 4, 5), A.add)
+    ts(col(8), col(7), 1.0, A.add, col(6), A.mult)
+    ts(v("ends", 0, 1), col(8), -1.0, A.add)
 
     for t in range(RO):
         last = t == RO - 1
         z = "zl" if t == 0 else "ys%d" % (t - 1)
         ys, yl, qu, ql, ks, kl, ns, nl, ws, wl = ["%s%d" % (k, t) for k in ("ys", "yl", "qu", "ql", "ks", "kl", "ns", "nl", "ws", "wl")]
-        Ls, hs, es = "Ls", "hs", "es"
-        oh, ohc, ohl = v(hs, 0, 256), v(hs, 256, 512), v(hs, 512, 768)
 
-        def pgather(c, tt_):
-            a, b = CH[c]
-            gather(PENG[c], v("G32" if PENG[c] == "act" else "G16", 16 * a, 16 * b), Pc, v("Rl%d" % tt_, a, b))
+        TAG[0] = "P%d" % t
+        for (a, b, e) in PG if t else PG0:
+            gather(e, v("G16", 16 * a, 16 * b), Pw, v("Rl%d" % t, a, b))
             inturn("g")
-
-        def diag(c):
-            a, b = CH[c]
-            gb, dg = ("G32", "dg32") if PENG[c] == "act" else ("G16", "dg16")
-            mms([(ps(1 + c, 0, b - a), blk(dg, k), v(gb, 16 * a + k, 16 * b, 16)) for k in range(16)])
-
-        def chain1(c):
-            a, b = CH[c]
-            n, bk = b - a, 1 + c
-            ts(v("fB", a, b), ps(bk, 0, n), 0.0, A.is_equal, BIG, A.mult)
-            ts(v(Ls, a, b), ps(bk, 0, n), -1.0, A.mult, float(W), A.add)
-            mms([(ps(bk, 128, 128 + n), M1, v("fB", a, b)), (ps(bk, 128, 128 + n), idh, v("R1", a, b))])
-            mms([(ps(bk, 128 + n, 128 + 2 * n), idh, v("fB", a, b)), (ps(bk, 128 + n, 128 + 2 * n), idh, v("R1", a, b))])
-
-        def chain2(c):
-            a, b = CH[c]
-            n, bk = b - a, 1 + c
-            ts(v("uw", 2 * a, 2 * b), ps(bk, 128, 128 + 2 * n), -BIG, A.add, 0.0, A.max)
-            mms([(ps(bk, 384, 384 + n), idhn, v("fB", a, b)), (ps(bk, 384, 384 + n), onh, v("uw", 2 * a, 2 * a + n))])
-
-        def chain3(c):
-            a, b = CH[c]
-            n, bk = b - a, 1 + c
-            tt(v("ix", a, b), ps(bk, 384, 384 + n), v("uw", 2 * a + n, 2 * b), A.max)
-            ts(v("ixu", a, b), v("ix", a, b), float(XO - 1), A.add)
-
-        def xgather(c):
-            a, b = CH[c]
-            gather(XENG[c], v("xg", 16 * a, 16 * b), v("X"), v("ixu", a, b))
+        for c in (1, 0):
+            a, b = 128 * c, 128 * c + 128
+            o = ps(c, 0, 128)
+            mms([(o, idh, blk("R1", c))] + [(o, dg(k), v("G16", 16 * a + k, 16 * b, 16)) for k in range(16)])
+            relu(ENG["u2"], blk("u2", c), o, -BIG * W)
+            ts(blk("Ls", c), o, 1.0 / BIG, A.mult, PAD - 0.2501, A.add)
+            mms([(ps(3 + c, 0, 128), M1, blk("u2", c))])
+            relu(ENG["u1"], blk("u1", c), ps(3 + c, 0, 128))
+            mms([(ps(3 + c, 128, 256), idN4, blk("u2", c)), (ps(3 + c, 128, 256), onh, blk("u1", c))])
+            tt(blk("ix", c), ps(3 + c, 128, 256), blk("u2", c), A.max)
+            ts(blk("ixu", c), blk("ix", c), PAD - 1.0, A.add)
+        ts(v("L1"), v("Ls"), 1.0 - PAD, A.add)
+        mms([(ps(6, 0, 256), idb, v(z)), (ps(6, 0, 256), onN, v("u2"))])
+        act(v("zz"), ps(6, 0, 256), AF.Relu, scale=2.0)
+        TAG[0] = "X%d" % t
+        for (a, b, e) in XG if t else XG0:
+            gather(e, v("xg", 16 * a, 16 * b), Xw, v("ixu", a, b))
             inturn("x")
-
-        def scans(c):
-            a, b = CH[c]
             n = 16 * (b - a)
-            scan(v("smx", 16 * a, 16 * b), v("rs0", 0, n), v("xg", 16 * a, 16 * b), A.mult, A.max)
-            scan(v("smn", 16 * a, 16 * b), v("rb", 0, n), v("xg", 16 * a, 16 * b), A.add, A.min)
-
-        def ymake(a, b, bk):
-            o = ps(bk, 0, b - a)
-            mms([(o, idb, v("ct", 0, b - a)), (o, idb, v("zz", a, b)),
-                 (o, idhalf, v("smx", 16 * a + 15, 16 * b, 16)), (o, idhalf, v("smn", 16 * a + 15, 16 * b, 16))])
-            ts(v(ys, a, b), o, MAGIC, A.add, -MAGIC, A.add)
-
-        if t == 0:
-            consts_a(); consts_b(); consts_c()
-        for c in range(len(CH)):
-            pgather(c, t); diag(c); chain1(c); chain2(c); chain3(c); xgather(c); scans(c)
-            a, b = CH[c]
-            act(v("Lf", a, b), ps(1 + c, 0, b - a), AF.Identity, bias=float(W), scale=-1.0)
-        mms([(ps(6, 0, 256), onn, v("fB")), (ps(6, 0, 256), idb, v(z))])
-        act(v("zz"), ps(6, 0, 256), AF.Relu)
+            scan(v("smx", 16 * a, 16 * b), v("rs0", 0, n), v("xg", 16 * a, 16 * b), A.min, A.max)
+            scan(v("smn", 16 * a, 16 * b), v("rb", 0, n), v("xg", 16 * a, 16 * b), A.max, A.min)
         if t > 0:
-            tt(ind(XC, v("wl%d" % (t - 1))), v("nl%d" % (t - 1), 0, 256), v("nl%d" % (t - 1), 256, 512), A.add)
-        cp(v("xq"), ind(XC, v("q0") if t == 0 else v("qu%d" % (t - 1))))
-        mms([(ps(7, 256, 272), wnd("oto", k), v("xq", k, 256, 16)) for k in range(16)])
+            scatter(XCw, "wl%d" % (t - 1), "nl%d" % (t - 1), DOWN, "cw%d" % t)
+        gather(ENG["xq"], v("xq"), XCw, v("q0") if t == 0 else v("qu%d" % (t - 1)))
+        o = ps(6, 256, 272)
+        mms([(o, idh, v("c256"))] + [(o, v("oto", 15 - k, 143 - k), v("xq", k, 256, 16)) for k in range(16)])
+        tt(v("D0", 0, 256, 16), o, v("si", 16, 32), A.max)
         mms([(ps(7, 0, 256), onh, v("xq"))])
-        ts(v("sm", 32, 48), ps(7, 256, 272), 0.0, A.is_equal)
         act(v("orow"), ps(7, 0, 256), AF.Relu, bias=1.0, scale=-1.0)
-        ts(v("sm", 48, 64), v("sm", 32, 48), -1.0, A.mult, 1.0, A.add)
-        tt(v("sm", 64, 80), v("sm", 48, 64), v("sm", 0, 16), A.mult)
-        tt(v("sm", 80, 96), v("sm", 64, 80), il8, A.add)
-        act(ps(1, 256, 512), v("Lf"), AF.Identity, bias=1.0)
 
-        for (a, b, bk) in ((0, YCUT, 5), (YCUT, 256, 6)):
-            ymake(a, b, bk)
-            a1, b1 = a // 16, b // 16
-            o = ps(bk, 256 + a1, 256 + b1)
-            mms([(o, wnd("sto", k), v(ys, a + k, b, 16)) for k in range(16)])
-            cp(v("si", a1, b1), o)
-            ts(v("si", 16 + a1, 16 + b1), v("si", a1, b1), 7, A.bitwise_and)
-            tt(v("sm", 96 + a1, 96 + b1), v("si", 16 + a1, 16 + b1), v("sm", 32 + a1, 32 + b1), A.mult)
-            tt(v("sm", 112 + a1, 112 + b1), v("sm", 96 + a1, 96 + b1), v("sm", 80 + a1, 80 + b1), A.add)
-            cp(v(qu, a1, b1), v("sm", 112 + a1, 112 + b1))
-            cp(ind(XC, v(qu, a1, b1)), v(ys, a, b))
+        TAG[0] = "Q%d" % t
+        for (a, b), bk in zip(YC, (2, 5)):
+            n, a1, b1 = b - a, a // 16, b // 16
+            oy, oq = ps(bk, 0, n), ps(bk, 256, 256 + n)
+            ends = [v("zz", a, b), v("smx", 16 * a + 15, 16 * b, 16), v("smn", 16 * a + 15, 16 * b, 16)]
+            mms([(oy, idb, v("cq", 0, n)), (oq, idb, v("OFF", a, b)), (oq, idb, v("ramp", a, b)), (oq, idb, v("cq", 0, n)), (oq, onB, v("xq", a, b))]
+                + [x for r in ends for x in ((oq, s0h, r), (oy, idhalf, r))])
+            scan(v("sq", a, b), v("D0", a, b), oq, A.max, A.min)
+            ts(v(ys, a, b), oy, MAGIC, A.add, -MAGIC, A.add)
+            cp(v("si", a1, b1), v("sq", a + 15, b, 16))
+            ts(v("si", 16 + a1, 16 + b1), v("si", a1, b1), 7 + 15 * 512, A.bitwise_and)
+            tt(v("qf", a1, b1), v("si", 16 + a1, 16 + b1), v("il8", a1, b1), A.add)
+            cp(v(qu, a1, b1), v("qf", a1, b1))
+            cp(ind(XCw, v(qu, a1, b1)), v(ys, a, b), chain="cq%d" % t)
         msg(v(ys), DC, v(yl), "my%d" % t)
         msg(v(qu), DC, v(ql), "mq%d" % t)
         if last:
             msg(v(ys), -DB, v("zol"), "mzo")
             dma("sync", T.zo[:], ap(v("zol")), [v("zol")], [], "st")
-
-        for (a, b, e) in ECH:
-            gather(e, v("eg", 16 * a, 16 * b), XC, v(Ls, a, b))
+        for h in (1, 0):
+            mms([(ps(6, 0, 128), blk(ys, h), idb)])
+            lin("act", blk("yT", h), ps(6, 0, 128), YOFF)
+            lin("act", blk("yp", h), blk(ys, h), EOFF)
+            mms([(ps(7, 0, 128), id8, blk(ys, h)), (ps(7, 0, 128), ido, blk("orow", h))])
+            act(blk("U8", h), ps(7, 0, 128), AF.Abs)
+        mms([(ps(6, 0, 256), idh, v("R1")), (ps(6, 0, 256), idb, v("U8"))])
+        lin(ENG["RU"], v("RU"), ps(6, 0, 256), BIG)
         if not last:
-            tt(v("sm", 0, 16), v("sm", 112, 128), il8, A.subtract)
-            ts(v("qh", 0, 16), v("sm", 112, 128), -1.0, A.mult, float(W), A.add)
-        cp(ind(Xc, v(ql)), v(yl))
-
-        def dfill(j):
-            h, kq, bk = j // 4, j % 4, 2 + j % 4
-            for kk in range(4):
-                k = 4 * kq + kk
-                o = ps(bk, 128 * kk, 128 * kk + 128)
-                mms([(o, idn, v(ys, 128 * h, 128 * h + 128)), (o, idb, v("eg", 2048 * h + k, 2048 * h + 2048, 16))])
-
-        def dread(j):
-            bk = 2 + j % 4
-            ts(v("ge", 512 * j, 512 * j + 512), ps(bk), 0.0, A.is_ge)
-            act(v("ab", 512 * j, 512 * j + 512), ps(bk), AF.Abs)
-
-        def dsum(j):
-            h, kq = j // 4, j % 4
-            if kq == 0:
-                mm(ps(6 + h, 0, 256), idb, v("cV"), True, False)
-            for kk in range(4):
-                k = 4 * kq + kk
-                mm(ps(6 + h, k, 256, 16), blk("ge", 4 * j + kk), v("Gn", 0, 16), False, False)
-            for kk in range(4):
-                k = 4 * kq + kk
-                mm(ps(6 + h, k, 128, 16), blk("ab", 4 * j + kk), v("Gn", 16, 24), False, kq == 3 and kk == 3)
-
-        def settle(h):
-            act(v("tB", 128 * h, 128 * h + 128), ps(6 + h, 128, 256), AF.Abs, bias=-7.5 * BV)
-            tt(v("km", 128 * h, 128 * h + 128), ps(6 + h, 0, 128), v("tB", 128 * h, 128 * h + 128), A.min)
-
-        for j in range(4):
-            dfill(j)
-        for j in range(8):
-            dread(j)
-            if j + 4 < 8:
-                dfill(j + 4)
-            dsum(j)
-        settle(0)
-        settle(1)
-        scan(v("S"), v("pot"), v("km"), A.add, A.max)
-        ts(v("si", 32, 48), v("S", 15, 256, 16), 1.0 - 2 * BV, A.add, 0.0, A.max)
-        ts(v("si", 48, 64), v("si", 32, 48), 511, A.bitwise_and)
-        cp(v("sp", 0, 256, 16), v("si", 48, 64))
-        scan(v("rep"), v("rs0", 0, 256), v("sp"), A.mult, A.add)
-        mms([(ps(2, 256, 512), idh, R1)])
-        mms([(ps(5, 0, 256), id8, v(ys)), (ps(5, 0, 256), ido, v("orow"))])
-        act(v("U8"), ps(5, 0, 256), AF.Abs)
-        mm(ps(0), idh, v("R1"), True, False)
-        mm(ps(0, 0, 256), idb, v("U8"), False, False)
-        mm(ps(0, 256, 512), idb, v("U8"), False, False)
-        mm(ps(0, 256, 512), v("id32"), v("Lf"), False, False)
-        if t == 1:
-            mms([(ps(3, 288, 304), shf, v("qh", 0, 16))])
-            cp(v("qh", 16, 32), ps(3, 288, 304))
-        if not last:
+            ts(v("qh"), v("qf"), -1.0 / BIG, A.mult, (W + PAD) / BIG, A.add)
             for k in range(16):
-                mms([(ps(5, k, 256, 16), blk("dg16", (k + t) % 16), v("qh", 16 * t, 16 * t + 16))])
-            act(v("Qd"), ps(5, 0, 256), AF.Copy)
-        for h in range(2):
-            mms([(ps(1, 128 * h, 128 * h + 128), v("rep", 128 * h, 128 * h + 128), idh)])
-        for j, thr in ((0, 8.5), (2, 2.5), (1, 3.0)):
-            act(v("a123", 256 * j, 256 * j + 256), ps(1, 0, 256), AF.Abs, bias=col(3 + j))
-            ts(v(hs, 256 * j, 256 * j + 256), v("a123", 256 * j, 256 * j + 256), thr, A.is_le)
+                mms([(ps(5, 256 + k, 512, 16), dg(k, t), v("qh"))])
+            lin(ENG["cap"], v("cap"), ps(5, 256, 512), float(W), -1.0)
 
-        tt(v("key"), ps(1, 256, 512), ohl, A.mult)
-        tt(v("key5"), ps(2, 256, 512), oh, A.mult)
-        e4, e5 = (EL4, EL5) if last else (EACT4, EACT5)
-        keys("", 3, 6, e4)
-        keys("5", 2, 7, e5)
-        ts(v("su", 32, 48), v("cl5", 0, 16), -1.0, A.add)
-        mms([(ps(1, 0, 16), wnd("kto", k), v(hs, 256 + k, 512, 16)) for k in range(16)])
-        tt(v("sm", 128, 144), ps(1, 0, 16), il16, A.add)
-        cp(v("su", 0, 16), v("sm", 128, 144))
-        gather("act", v(es), v("eg"), v("su", 0, 16))
-        mm(ps(0, 0, 256), idN, ohc, False, False)
-        mm(ps(0, 256, 512), idB, ohc, False, True)
-        act(v("v2"), ps(0, 256, 512), AF.Identity, bias=1.0 - BIG)
-        tt(v("vi"), ps(0, 0, 256), v("v2"), A.max)
-        ts(v("vj"), v("vi"), W - 1, A.bitwise_and)
-        cp(v("Rl%d" % (t + 1)), v("vj"))
-        ops[-1]["first"] = 0.0 if last else FIRST
-        if last:
-            msg(v("Rl3"), -DB, v("rol"), "mro")
-        else:
-            ts(R1, v("vj"), 1.0, A.add)
-            gather("act", v("oP"), Pc, v("su", 32, 48))
-            o = ps(6, 0, 256)
-            mms([(o, idb, v("MB", 256 * t, 256 * t + 256)), (o, idN, ohc), (o, idN, ohl), (o, v("id32"), v("oP"))])
-            act(v("bP"), o, AF.Relu)
-        dedupe("", 3, 4, e4, [(ps(4, 0, 256), onh, v("ch")), (ps(4, 0, 256), onN, ohl)])
-        places(4, "sc4", v(ks))
-        msg(v(ks), DC, v(kl), "mk%d" % t)
-        dedupe("5", 2, 5, e5, [])
-        places(5, "sc", v(ws))
+        TAG[0] = "E%d" % t
+        for (a, b, e) in EG:
+            gather(e, v("eg", 16 * a, 16 * b), XCw, v("Ls", a, b), EOFF)
+            inturn("e")
+        for h in range(2):
+            cp(ind(Xw, blk(ql, h, 8)), blk(yl, h))
+        for h in (1, 0):
+            TAG[0] = "E%d%d" % (t, h)
+            bk = 4 - h
+            s0, s32, s1, s8 = [blk("st", 4 * h + j) for j in range(4)]
+            R1, L1 = blk("R1", h), blk("L1", h)
+            ba = 2 if h else 7
+            mms([(ps(ba, 0, 256), blk("yp", h), v("YS", 0, 256))], stop=False)
+            mms([(ps(bk, 256, 512), blk("yp", h), v("YS", 256, 512)), (ps(bk, 384, 512), idb, v("cV"))]
+                + [(ps(bk, 384 + k, 512, 16), v("eg", 2048 * h + k, 2048 * h + 2048, 16), v("GE")) for k in range(16)], stop=False)
+            for j in range(4):
+                mms([(ps(j % 2), blk("yT", h), blk("EX", j, 512))])
+                tt(blk("Mx", 4 * h + j, 512), blk("eg", 4 * h + j, 512), ps(j % 2), A.max)
+            mms([(ps(ba, k, 256, 16), v("Mx", 2048 * h + k, 2048 * h + 2048, 16), v("GM", 0, 16)) for k in range(16)], start=False)
+            mms([(ps(bk, 256 + k, 512, 16), v("Mx", 2048 * h + k, 2048 * h + 2048, 16), v("GM", 16, 32)) for k in range(16)], False, False)
+            ts(blk("Pr", h, 256), ps(ba, 0, 256), MAGIC, A.add, -MAGIC, A.add)
+            mms([(ps(bk, 256, 384), idn16, blk("Pr", 2 * h)), (ps(bk, 256, 384), idn16, blk("Pr", 2 * h + 1)),
+                 (ps(bk, 384, 512), id1008, blk("Pr", 2 * h)), (ps(bk, 384, 512), id1008, blk("Pr", 2 * h + 1))], start=False)
+            act(blk("tB", h), ps(bk, 256, 384), AF.Abs, bias=8.5 * BV, scale=BV)
+            tt(blk("km", h), ps(bk, 384, 512), blk("tB", h), A.min)
+            scan(blk("S", h), v("pot"), blk("km", h), A.add, A.max)
+            ts(v("si", 32 + 8 * h, 40 + 8 * h), v("S", 128 * h + 15, 128 * h + 128, 16), 17.0 - 2 * BV, A.add, 0.0, A.max)
+            ts(v("si", 48 + 8 * h, 56 + 8 * h), v("si", 32 + 8 * h, 40 + 8 * h), 511, A.bitwise_and)
+            ts(v("sp", 128 * h, 128 * h + 128, 16), v("si", 48 + 8 * h, 56 + 8 * h), -480.0, A.add)
+            scan(blk("rep", h), v("rs0", 0, 128), blk("sp", h), A.min, A.add)
+            for o, c in ((s0, 0.0), (s32, 32.0), (s1, 1.0), (s8, 8.0)):
+                ts(o, blk("rep", h), c, A.is_ge)
+
+            TAG[0] = "T%d%d" % (t, h)
+            for j in ((1, 0) if last else (0, 1)):
+                bK, bT, bD = (((1, 4, 7), (0, 0, 2)), ((5, 3, 2), (6, 5, 5)))[h][j]
+                u = 2 * h + j
+                K, cT, o = blk("KK", u), v("cT", 128 * u, 128 * u + 128, 1, 8), ps(bK, 0, 128)
+                mms([(o, idh, (R1, L1)[j]), (o, (s0, s1)[j], idB8), (o, (s32, s8)[j], idN8)])
+                relu(ENG["K"][u], K, o, -BIG8)
+                for m in range(16):
+                    mms([(ps(bT, 128 + m, 256, 16, 8), v("KK", 128 * u + m, 128 * u + 128, 16), v("Gn"))])
+                lin(ENG["cT"][u], cT, ps(bT, 128, 256, 1, 8))
+                if j == 0:
+                    mms([(ps(bk, 256, 264), cT, v("idh", 0, 8, 1, 8))])
+                    if not last:
+                        o = ps(bk, 384, 512)
+                        mms([(o, idb, v("MB", t, t + 128)), (o, s1, idB8), (o, s32, idN8)], stop=False)
+                    ts(v("tl", 8 * h, 8 * h + 8), ps(bk, 256, 264), PAD - 1.0, A.add)
+                rows = [(ps(bD, SEG[r] + 16 * (r + 1) * q, SEG[r] + 16 * (r + 1) * (q + 1) - 1), onB,
+                         v("KK", 128 * u + 64 * q, 128 * u + 64 * q + 16 * r + 15)) for r in range(4) for q in range(2)]
+                o = ps(bD, 0, 320)
+                if h:
+                    mms([(o, v("cT", 128 * u, 128 * u + 128, 1, 48), v("SEL", 0, 320, 1, 48))] + rows)
+                else:
+                    mms([(o, v("cT", 512, 640, 1, 48), v("SEL", 0, 320, 1, 48))] + rows + [(o, cT, v("SEL", 0, 320, 1, 8))])
+                act(blk("AD", u, 320), o, AF.Abs)
+                scan(blk("sc", u, 320), v("RS"), blk("AD", u, 320), A.add, A.min)
+                cp(blk((ws, ks)[j], h, 16), ind(blk("sc", u, 320), v("ends", 0, 1)))
+            if not last:
+                gather(ENG["oP"], blk("oP", h), Pw, v("tl", 8 * h, 8 * h + 8))
+                mms([(ps(bk, 384, 512), idh, blk("oP", h))], start=False)
+                tt(blk("nP", h), ps(bk, 384, 512), blk("cap", h), A.min)
+            od, ou = ps(5, 384, 512), ps(6, 128, 256)
+            mms([(ou, idh, L1), (ou, idb, blk("U8", h)), (ou, s8, idB8), (ou, s32, idN8)])
+            tt(blk("vi", h), ou, blk("RU", h), A.max)
+            ts(blk("vj", h), blk("vi", h), W - 1, A.bitwise_and)
+            if not last:
+                ts(blk("Rl%d" % (t + 1), h), blk("vj", h), float(PAD), A.add)
+            mms([(od, idh, L1), (od, idhn, R1), (od, s8, idB8), (od, s32, idN8)])
+            relu("act", blk("D32", h), od, TW - BIG8)
+            lin("act", blk("Rf", h) if last else R1, blk("vj", h), 0.0 if last else 1.0)
+            for m in range(16):
+                o = ps(bk, m, 128, 16, 8)
+                mms([(o, v("KK", 256 * h + m, 256 * h + 128, 16), v("Gn")), (o, v("D32", 128 * h + m, 128 * h + 128, 16), v("Gn32"))])
+            cT3 = v("cT3", 128 * h, 128 * h + 128, 1, 8)
+            lin("act", cT3, ps(bk, 0, 128, 1, 8))
+            mms([(ps(bk, 256, 264), cT3, v("id32", 0, 8, 1, 8))])
+            ts(v("tl", 16 + 8 * h, 24 + 8 * h), ps(bk, 256, 264), PAD - 1.0, A.add)
+
+        TAG[0] = "S%d" % t
         if not last:
+            scatter(Pw, ws, "nP", DOWN, "p%d" % t)
+        for h in (1, 0):
+            msg(v(ks, 16 * h, 16 * h + 8), DC, v(kl, 16 * h, 16 * h + 8), "m%s%d" % ("kj"[h], t))
+        if last:
+            msg(v("Rf"), -DB, v("rol"), "mro")
+            dma("sync", T.ro[:], ap(v("rol")), [v("rol")], [], "st")
+        else:
             msg(v(ws), -DC, v(wl), "mw%d" % t)
-            tt(ind(v("P"), v(ws)), v("bP"), v("Qd"), A.add)
-            ops[-1]["first"] = FIRST
-            cp(ind(XC, v(ks)), c0)
-        cp(ind(Xc, v(kl)), c0)
-        gather("act", v("oX"), Xc, v("su", 32, 48))
-        o = ps(7, 0, 256)
-        mms([(o, idb, cq), (o, idhalf, v(es)), (o, onB, ohc), (o, idhalf, v("oX"))])
-        o = ps(1, 256, 512)
-        mms([(o, onN, ohc), (o, idb, v("oX"))])
-        act(v("aa"), ps(7, 0, 256), AF.Identity, bias=MAGIC - BIG)
-        ts(v(ns, 256, 512), ps(1, 256, 512), 0.0, A.max)
-        act(v(ns, 0, 256), v("aa"), AF.Relu, bias=-MAGIC)
-        tt(ind(Xc, v(ws)), v(ns, 0, 256), v(ns, 256, 512), A.add)
+        scatter(Xw, kl, None, DOWN, "xk%d" % t)
+        for j in range(2):
+            gather(ENG["oX"][j], blk("oX", j, 256), XX, blk("tl", j, 16))
+        if not last:
+            scatter(XCw, ks, None, DOWN, "ck%d" % t)
+        o = ps(7, 256, 512)
+        mms([(o, idb, cq), (o, idhalf, v("oX", 256, 512)), (o, idhalf, v("oX", 0, 256))])
+        ts(v(ns), o, MAGIC, A.add, -MAGIC, A.add)
+        scatter(Xw, ws, ns, DOWN, "xw%d" % t)
         if not last:
             msg(v(ns), -DC, v(nl), "mn%d" % t)
 
-    dma("sync", T.xo[:, 0:1024], ap(v("X", XO, XO + 1024)), [v("X")], [], "st")
-    dma("act", T.xo[:, 1024:2048], ap(v("X", XO + 1024, XO + 2048)), [v("X")], [], "st")
-    cp(v("rof"), v("rol"))
-    dma("sync", T.ro[:], ap(v("rof")), [v("rof")], [], "st")
+    dma("sync", T.xo[:, 0:1024], ap(v("XX", PAD, PAD + 1024)), [Xw], [], "st")
+    dma("act", T.xo[:, 1024:2048], ap(v("XX", PAD + 1024, TW)), [Xw], [], "st")
 
     n = len(ops)
     succ = [[] for _ in range(n)]
@@ -568,26 +545,61 @@ def rank_program(g, core, T, topo):
     for k in range(n - 1, -1, -1):
         o = ops[k]
         prio[k] = o["cost"] + o.get("first", 0.0) + max([0.0] + [prio[j] + (o["lat"] + HOP if k in ops[j]["deps"] else 0.0) for j in succ[k]])
-    est = [0.0] * n
-    free = {}
-    ready = [k for k in range(n) if left[k] == 0]
-    seq = []
-    while ready:
-        def start(k):
-            return max(est[k], free.get(ops[k]["q"], 0.0))
-        k0 = min(ready, key=lambda k: (start(k), -prio[k]))
-        lim = start(k0) + WIN * ops[k0]["cost"]
-        k = max([j for j in ready if ops[j]["q"] == ops[k0]["q"] and start(j) <= lim], key=lambda j: (prio[j], -j))
-        ready.remove(k)
-        seq.append(k)
-        o = ops[k]
-        end = start(k) + o["cost"]
-        free[o["q"]] = end if o["q"] != "land" else 0.0
-        for j in succ[k]:
-            est[j] = max(est[j], end + (o["lat"] + HOP if k in ops[j]["deps"] else 0.0))
-            left[j] -= 1
-            if left[j] == 0:
-                ready.append(j)
+    pred = [[(j, ops[j]["lat"] + HOP if j in o["deps"] else 0.0) for j in set(o["deps"]) | set(o["order"])] for o in ops]
+    post = [[(j, ops[k]["lat"] + HOP if k in ops[j]["deps"] else 0.0) for j in succ[k]] for k in range(n)]
+
+    def place(order, before, tail):
+        end = [0.0] * n
+        busy = {}
+        for k in order:
+            o = ops[k]
+            s = max([tail[k]] + [end[j] + d for j, d in before[k]])
+            if o["q"] != "land":
+                b = busy.setdefault(o["q"], [])
+                i = len(b)
+                while i > 0 and b[i - 1][1] > s:
+                    i -= 1
+                while i < len(b) and b[i][0] < s + o["cost"]:
+                    s = max(s, b[i][1])
+                    i += 1
+                b.insert(i, (s, s + o["cost"]))
+            end[k] = s + o["cost"]
+        return end
+
+    if not ORDER:
+        order = sorted(range(n), key=lambda k: (-prio[k], k))
+        best = None
+        for _ in range(SWEEPS):
+            end = place(order, pred, [0.0] * n)
+            span = max(end[k] + ops[k]["lat"] for k in range(n))
+            SPAN.append(round(span))
+            if best is None or span < best:
+                best = span
+                ORDER[:] = sorted(range(n), key=lambda k: (end[k] - ops[k]["cost"], k))
+            back = place(sorted(range(n), key=lambda k: (-end[k], -k)), post, [o["lat"] for o in ops])
+            order = sorted(range(n), key=lambda k: (-back[k], k))
+        seed = [1]
+
+        def draw(m):
+            seed[0] = (seed[0] * 1103515245 + 12345) % 2147483648
+            return (seed[0] >> 8) % m
+        end = place(ORDER, pred, [0.0] * n)
+        key = [end[k] - ops[k]["cost"] for k in range(n)]
+        for _ in range(SHAKES):
+            amp, mid, wide = (100, 300, 1000, 3000)[draw(4)], draw(int(best)), (3000, 10000, 40000)[draw(3)]
+            k2 = [x + (draw(2 * amp) - amp if abs(x - mid) < wide and draw(10) < 3 else 0) for x in key]
+            for k in range(n):
+                k2[k] = max([k2[k]] + [k2[j] for j, d in pred[k]])
+            end = place(sorted(range(n), key=lambda k: (k2[k], k)), pred, [0.0] * n)
+            back = place(sorted(range(n), key=lambda k: (-end[k], -k)), post, [o["lat"] for o in ops])
+            end = place(sorted(range(n), key=lambda k: (-back[k], k)), pred, [0.0] * n)
+            span = max(end[k] + ops[k]["lat"] for k in range(n))
+            if span <= best:
+                best = span
+                key = [end[k] - ops[k]["cost"] for k in range(n)]
+                ORDER[:] = sorted(range(n), key=lambda k: (key[k], k))
+                SPAN.append(round(span))
+    seq = ORDER
     pos = {k: i for i, k in enumerate(seq)}
     need = set()
     for o in ops:
@@ -612,6 +624,7 @@ def rank_program(g, core, T, topo):
             if seen[q].get(sem, 0) < val:
                 eng[q].wait_ge(T.sem[sem], val)
                 seen[q][sem] = val
+        TAG[0] = o["tag"]
         r = o["fn"]()
         if k in need:
             total[q] = total.get(q, 0) + 1

from concourse.mybir import AluOpType, ActivationFunctionType

N, W, E, RO, DB, DC = 8, 2048, 256, 3, 3, 2
PAD = 80
TW = PAD + W
BIG, BIG8 = 4096.0, 8192.0
BV = float(1 << 22)
MAGIC = 12582912.0
EOFF, YOFF = -127.5, -127.5625
PG0 = [(128, 192, "dve"), (192, 256, "act"), (0, 48, "dve"), (48, 128, "act")]
PG = [(128, 192, "dve"), (192, 256, "act"), (0, 64, "act"), (64, 128, "act")]
XG0 = [(192, 256, "act"), (128, 192, "act"), (96, 128, "dve"), (32, 96, "act"), (0, 32, "act")]
XG = [(192, 256, "act"), (128, 192, "act"), (64, 128, "act"), (32, 64, "act"), (0, 32, "act")]
YC = [(64, 256), (0, 64)]
EG = [(128, 160, "dve"), (160, 192, "act"), (192, 224, "act"), (224, 256, "act"), (0, 32, "act"), (32, 64, "act"), (64, 96, "act"), (96, 128, "act")]
ENG = {"u2": "dve", "u1": "dve", "K": ["act"] * 4, "cT": ["act"] * 4, "xq": "act", "RU": "act", "cap": "act", "oP": "act", "oX": ("dve", "act")}
CYC, GAT, SCA, PEC, FIX, FIXA, FIXP, HOP, FAR, BW = 1.04, 1.56, 3.8, 0.525, 30.0, 60.0, 5.0, 60.0, 3000.0, 60.0
START = 4000.0
SPAN = []
TAG = [""]
SEG = [16 * r * (r + 1) for r in range(4)]
ORDER = []
SWEEPS = 3
SHAKES = 1200

F, H, B, I, U = "float32", "float16", "bfloat16", "int32", "uint16"
BUFS = [
    ("XX", 2 * TW + 16, B), ("P", TW, I), ("rdi", 256, I), ("r0s", 256, U), ("z0s", 256, B), ("zl", 256, B),
    ("R1", 256, H), ("G16", 4096, H), ("u2", 256, H), ("u1", 256, H), ("ix", 256, H), ("ixu", 256, U), ("Ls", 256, U), ("L1", 256, H),
    ("xg", 4096, B), ("smx", 4096, B), ("smn", 4096, B), ("zz", 256, B), ("xq", 256, H), ("orow", 256, B), ("D0", 256, F),
    ("sq", 256, F), ("si", 64, I), ("qf", 16, F), ("qh", 16, H), ("yp", 256, H), ("yT", 256, H), ("U8", 256, B), ("cap", 256, H),
    ("eg", 4096, B), ("Mx", 4096, H), ("Pr", 512, H), ("tB", 256, F), ("km", 256, F), ("S", 256, F), ("sp", 256, H), ("rep", 256, H),
    ("st", 1024, H), ("KK", 512, H), ("D32", 256, F), ("RU", 256, F), ("vi", 256, I), ("vj", 256, I), ("cT", 768, H), ("cT3", 256, F), ("tl", 32, U),
    ("AD", 1280, F), ("sc", 1280, F), ("ends", 2, U), ("oP", 256, H), ("nP", 256, F), ("oX", 512, B), ("Rf", 256, F), ("rol", 256, F), ("zol", 256, B),
    ("pj", 144, F), ("jg", 128, F), ("jk", 256, F), ("ramp", 256, B), ("pi", 8, I), ("col", 16, F), ("km16", 16, F),
    ("id32", 128, F), ("idb", 128 * 5, B), ("idh", 128 * 8, H), ("onh", 128 * 3, H), ("one", 512, H),
    ("dg", 2080, H), ("EX", 2048, H), ("oto", 144, H), ("c256", 16, H), ("OFF", 256, B), ("MB", 144, B), ("rs0", 1024, B), ("rb", 1024, B),
    ("pot", 128, B), ("il8", 16, F), ("q0", 16, U), ("Gn", 8, H), ("Gn32", 8, F), ("GM", 32, H), ("GE", 8, B), ("YS", 512, H),
    ("cV", 128, B), ("cq", 256, B), ("c0", 64, B), ("SEL", 320, H), ("RS", 320, B), ("tmp", 512, F),
]
for _t in range(RO):
    BUFS += [("%s%d" % (_n, _t), _c, _d) for _n, _c, _d in [
        ("Rl", 256, U), ("ys", 256, B), ("yl", 256, B), ("qu", 16, U), ("ql", 16, U), ("ks", 32, U), ("kl", 32, U),
        ("ns", 256, B), ("nl", 256, B), ("ws", 32, U), ("wl", 32, U)]]
SCRATCH = {}
PLACE = {}
for _n, _c, _d in BUFS:
    if _c >= 1024:
        SCRATCH[_n] = ("sbuf", [128, _c], _d)
        PLACE[_n] = (_n, 0, _c)
    else:
        _p = "all_" + _d
        _o = SCRATCH[_p][1][1] if _p in SCRATCH else 0
        SCRATCH[_p] = ("sbuf", [128, _o + (_c + 15) // 16 * 16], _d)
        PLACE[_n] = (_p, _o, _c)
for _t in range(8):
    SCRATCH["ps%d" % _t] = ("psum", [128, 512], F)
    PLACE["ps%d" % _t] = ("ps%d" % _t, 0, 512)

SEMAPHORES = ["dve", "act", "pe", "pool", "sent", "st", "ld0", "ld1", "ld2", "ld3", "ld4", "mr", "mz", "mro", "mzo", "mx", "sx"] + \
    ["m%s%d" % (k, t) for t in range(RO) for k in ("y", "q", "k", "j", "n", "w")]


def rank_program(g, core, T, topo):
    rank = T.rank_of(core)
    if rank is None:
        return
    A = AluOpType
    AF = ActivationFunctionType
    ops = []
    acc = {}

    def v(name, a=0, b=None, s=1, n=128, p0=0):
        p, o, c = PLACE[name]
        return (p, o + a, o + (c if b is None else b), s, name, n, p0)

    def ind(win, off):
        return ("*", win, off)

    def ap(x):
        if x[0] == "*":
            return ap(x[1]).indirect(ap(x[2]))
        rows = slice(None) if x[5] == 128 else slice(x[6], x[6] + x[5])
        return T[x[0]][rows, x[1]:x[2]] if x[3] == 1 else T[x[0]][rows, x[1]:x[2]:x[3]]

    def arg(x):
        return ap(x) if isinstance(x, tuple) else x

    def rec(q, fn, reads, writes, tok=None, kind=None, chain=None):
        k = len(ops)
        deps, order = set(), set()
        rs, ws = [], []
        o = writes[0] if writes else None
        full = [x for x in reads if isinstance(x, tuple) and (x[0] == "*" or x[2] - x[1] > 1)]
        cost, lat = 60.0, 0.0
        if tok is not None:
            x = reads[0] if reads else (o if o else None)
            size = 128 * (x[2] - x[1]) * (4 if SCRATCH[x[0]][2] in (F, I) else 2)
            if q == "land":
                cost, lat = 0.0, FAR + size / BW + (START if TAG[0] == "init" else 0.0)
                order.add(k - 1)
            elif q == "pool":
                cost, lat = 400.0, FAR + size / BW
            else:
                cost, lat = (size / 250.0, 1800.0) if q == "sync" else (60.0, 1800.0 + size / 250.0)
        elif q == "pe":
            m = len(range(reads[0][1], reads[0][2], reads[0][3]))
            cost = FIXP + max(min(64, m), len(range(o[1], o[2], o[3]))) * PEC * (4 if SCRATCH[reads[0][0]][2] == F else 1)
        elif o[0] == "*":
            cost = 55 + 16 * (o[2][2] - o[2][1]) * SCA * CYC
        else:
            n = len(range(o[1], o[2], o[3]))
            if full and full[0][0] == "*":
                cost = 55 + n * GAT * CYC
            else:
                per = 2.0 if q == "pool" else 1.0
                if q == "dve" and kind == "tt":
                    per = 1.0 if any(SCRATCH[x[0]][0] == "psum" for x in full) else 2.0
                elif q == "dve" and all(SCRATCH[x[0]][2] in (H, B, U) for x in full + [o]):
                    per = 0.5
                cost = (FIXA if q == "act" else FIX) + max(64, n * per) * CYC + (100 if q == "pool" else 0)
        for x in reads:
            if isinstance(x, tuple):
                rs += [x[1], x[2]] if x[0] == "*" else [x]
        for x in writes:
            if x[0] == "*":
                ws.append(x[1])
                rs.append(x[2])
            else:
                ws.append(x)
        for lst, wr in ((rs, False), (ws, True)):
            for x in lst:
                if SCRATCH[x[0]][0] == "psum":
                    ep = acc.setdefault(x[4], [None, [], []])
                    if ep[0] != q:
                        ep[0], ep[1], ep[2] = q, [], ep[1]
                    deps.update(a[2] for a in ep[2])
                    if q == "pe":
                        order.update(a[2] for a in ep[1][-1:])
                    else:
                        deps.update(a[2] for a in ep[1] if (wr or a[3]) and a[0] < x[2] and x[1] < a[1] and a[2] != k)
                    ep[1].append((x[1], x[2], k, wr))
                    continue
                rd_, wr_ = acc.setdefault(x[4], ([], []))
                deps.update(a[2] for a in (rd_ + wr_ if wr else wr_)
                            if a[0] < x[2] and x[1] < a[1] and a[3] < x[6] + x[5] and x[6] < a[4] and a[2] != k)
                if wr and x[3] == 1:
                    for z in (rd_, wr_):
                        z[:] = [a for a in z if not (x[1] <= a[0] and a[1] <= x[2] and x[6] <= a[3] and a[4] <= x[6] + x[5])]
                (wr_ if wr else rd_).append((x[1], x[2], k, x[6], x[6] + x[5]))
        if q == "sync":
            order.update(acc.get("*sync", []))
            acc["*sync"] = [k]
        ops.append({"q": q, "fn": fn, "deps": deps, "tok": tok, "order": order, "cost": cost, "lat": lat, "chain": chain, "tag": TAG[0]})

    def inturn(name):
        name = "*" + name + ops[-1]["q"]
        ops[-1]["order"].update(acc.get(name, []))
        acc[name] = [len(ops) - 1]

    def cp(out, in_, chain=None):
        rec("dve", lambda: g.vector.tensor_copy(ap(out), ap(in_)), [in_], [out], chain=chain)

    def tt(out, a, b, op):
        rec("dve", lambda: g.vector.tensor_tensor(ap(out), ap(a), ap(b), op), [a, b], [out], kind="tt")

    def ts(out, a, s1, op0, s2=None, op1=None):
        if op1 is None:
            rec("dve", lambda: g.vector.tensor_scalar(ap(out), ap(a), arg(s1), None, op0), [a, s1], [out])
        else:
            rec("dve", lambda: g.vector.tensor_scalar(ap(out), ap(a), arg(s1), arg(s2), op0, op1), [a, s1, s2], [out])

    def scan(out, d0, d1, op0, op1):
        rec("dve", lambda: g.vector.tensor_tensor_scan(ap(out), ap(d0), ap(d1), 0.0, op0, op1), [d0, d1], [out])

    def ms(out, c):
        rec("dve", lambda: g.vector.memset(ap(out), c), [], [out])

    def act(out, in_, func, bias=0.0, scale=1.0):
        rec("act", lambda: g.scalar.activation(ap(out), ap(in_), func, bias=arg(bias), scale=arg(scale)), [in_, bias, scale], [out])

    def mm(o, l, r, start, stop):
        rec("pe", lambda: g.tensor.matmul(ap(o), ap(l), ap(r), start, stop), [l, r], [o])

    def mms(lst, start=True, stop=True):
        for i, (o, l, r) in enumerate(lst):
            mm(o, l, r, start and i == 0, stop and i == len(lst) - 1)

    def iota(out, pat, base, cm):
        if SCRATCH[out[0]][2] == I:
            rec("pool", lambda: g.iota(ap(out), pat, base, cm), [], [out])
        else:
            rec("pool", lambda: g.iota(ap(out), pat, base, cm, allow_small_or_imprecise_dtypes=True), [], [out])

    def lin(eng, out, in_, bias=0.0, scale=1.0):
        if eng == "act":
            act(out, in_, AF.Identity, bias=bias, scale=scale)
        else:
            ts(out, in_, scale, A.mult, bias, A.add)

    def relu(eng, out, in_, bias=0.0):
        if eng == "act":
            act(out, in_, AF.Relu, bias=bias)
        else:
            ts(out, in_, bias, A.add, 0.0, A.max)

    def gather(eng, out, win, off, bias=None):
        if bias is not None:
            lin(eng, out, ind(win, off), bias)
        elif eng == "act":
            act(out, ind(win, off), AF.Copy)
        else:
            cp(out, ind(win, off))

    def scatter(win, lst, src, blocks, chain):
        for b in blocks:
            a = 16 * (b // 2) + 4 * (b % 2)
            cp(ind(win, v(lst, a, a + 4)), v("c0") if src is None else blk(src, b, 64), chain=chain)

    total = {}

    def dma(q, out, in_, reads, writes, sem):
        e = g.sync if q == "sync" else g.scalar
        total[sem] = total.get(sem, 0) + 16
        rec(q, lambda: e.dma_start(out, in_).then_inc(T.sem[sem], 16), reads, writes, tok=(sem, total[sem]))

    def msg(src, hop, dst, sem, part=None, own="sent"):
        to = T.cores[(rank + hop) % N]
        frm = T.cores[(rank - hop) % N]
        rid, pid, _ = topo.addr(to)

        def pick(a, b):
            e = topo.engines(a, b)
            return e if part is None else e[part::2]
        mask = sum(1 << e for e in pick(core, to))
        total[own] = total.get(own, 0) + len(pick(core, to))
        total[sem] = len(pick(frm, core))
        rec("pool", lambda: g.remote_dma(ap(dst), ap(src), T.sem[sem], T.sem[own], pid, rid, mask), [src], [],
            tok=(own, None if own == "sent" else total[own]))
        rec("land", None, [], [dst], tok=(sem, total[sem]))

    def ps(b, a=0, e=512, s=1, n=128):
        return v("ps%d" % b, a, e, s, n)

    def col(j):
        return v("col", j, j + 1)

    def blk(name, k, w=128):
        return v(name, w * k, w * k + w)

    Xw, XCw, XX, Pw = v("XX", 0, TW), v("XX", TW, 2 * TW + 16), v("XX"), v("P")
    idb, idhalf, id8, ido, s0h = [blk("idb", j) for j in range(5)]
    idh, idhn, idN4, idB8, idN8, idn16, id1008, M1 = [blk("idh", j) for j in range(8)]
    onh, onB, onN = [blk("onh", j) for j in range(3)]
    id32, cq = v("id32"), v("cq")
    DOWN = [3, 2, 1, 0]

    def dg(k, shift=0):
        a = 16 + 128 * k - (shift if k + shift < 16 else shift - 16)
        return v("dg", a, a + 128)

    TAG[0] = "init"
    dma("sync", ap(v("rdi")), T.rd[:], [], [v("rdi")], "ld0")
    dma("act", ap(v("z0s")), T.z0[:], [], [v("z0s")], "ld1")
    dma("sync", ap(v("XX", PAD, TW)), T.x0[:], [], [v("XX", PAD, TW)], "ld4")
    for j in range(2):
        o = v("P", PAD + 1024 * j, PAD + 1024 * j + 1024)
        dma("sync", ap(o), T.lk[:, 1024 * j:1024 * j + 1024], [], [o], "ld%d" % (2 + j))
    iota(v("pi", 0, 1), [[1, 1]], 0, 1)
    iota(v("pj"), [[1, 144]], 0, -1)
    iota(v("jk"), [[0, 16], [1, 16]], 0, 0)
    iota(v("jg"), [[1, 8], [0, 16]], 0, 0)
    ts(v("r0s"), v("rdi"), float(PAD), A.add)
    msg(v("r0s"), DB, v("Rl0"), "mr", 0)
    msg(v("z0s"), DB, v("zl"), "mz", 1)
    ops[-2]["order"].add(len(ops) - 4)
    ms(v("XX", 0, PAD), 0.0); ms(v("XX", TW, TW + PAD), 0.0); ms(v("XX", 2 * TW, 2 * TW + 16), 0.0); ms(v("P", 0, PAD), 0)
    msg(v("XX", PAD, TW), -DC, v("XX", TW + PAD, 2 * TW), "mx", own="sx")
    ops[-2]["order"].add(len(ops) - 8)
    ts(v("R1"), v("Rl0"), 1.0 - PAD, A.add)

    ts(v("pi", 1, 2), v("pi", 0, 1), 15, A.bitwise_and)
    ts(v("pi", 2, 3), v("pi", 0, 1), 4, A.arith_shift_right)
    cp(v("col", 0, 2), v("pi", 1, 3))
    ts(id32, v("pj", 0, 128), 0.0, A.is_equal)
    ts(v("km16"), v("jk", 0, 16), col(0), A.is_equal, BIG, A.mult)
    ms(cq, -0.25); ms(v("c0"), 0.0)
    for o, c in ((blk("one", 0, 256), -4.0), (blk("one", 1, 256), -4.0), (v("sp"), -128.0), (v("D0"), 4.0)):
        lin("act", o, cq, 0.0, c)
    ts(v("dg", 0, 16), v("cq", 0, 16), 0.0, A.mult); ts(v("dg", 2064, 2080), v("cq", 0, 16), 0.0, A.mult)
    for k in range(16):
        act(dg(k), id32, AF.Copy, scale=v("km16", k, k + 1))
    cp(idh, id32); cp(idb, id32)
    for o, c in ((idhn, -1.0), (idN4, -BIG), (idB8, BIG8), (idN8, -BIG8), (idn16, -16.0), (id1008, 1008.0)):
        ts(o, idh, c, A.mult)
    for o, c in ((idhalf, 0.5), (id8, 8.0), (ido, -2040.0)):
        ts(o, idb, c, A.mult)
    ts(onh, v("jg"), col(1), A.is_equal)
    ts(onB, onh, BIG, A.mult); ts(onN, onh, -BIG, A.mult)
    ts(v("tmp", 0, 128), v("jk", 0, 128), col(0), A.is_gt)
    tt(v("tmp", 128, 256), v("tmp", 0, 128), onN, A.mult)
    tt(M1, id32, v("tmp", 128, 256), A.add)
    ts(col(2), v("km16", 0, 1), 0.5 / BIG, A.mult)
    ts(s0h, onh, col(2), A.mult)
    iota(v("rs0"), [[0, 64], [256, 16]], 0, 0)
    lin("act", v("rb"), v("rs0"), 256.0, -1.0)
    for j in range(4):
        e = blk("EX", j, 512)
        rec("pool", lambda e=e, j=j: g.affine_select(ap(e), ap(v("one")), [[1, 32], [0, 16]], A.is_equal, 0.0, 32 * j, -1), [v("one")], [e])
    ts(col(3), col(0), -1.0, A.mult, 15.0, A.add)
    ts(v("oto"), v("pj"), col(3), A.is_equal, -256.0, A.mult)
    iota(v("ramp"), [[512, 16], [0, 16]], 0, 0)
    ramp = v("ramp", 0, 256, 16)
    ts(v("c256"), ramp, 256.0, A.add)
    ts(v("OFF"), v("jk"), col(0), A.not_equal, float(1 << 21), A.mult)
    ts(v("MB"), v("jk", 0, 144), col(0), A.is_equal, BIG8, A.mult)
    ms(v("pot"), 32.0); ms(v("pot", 0, 128, 16), -float(1 << 24))
    ts(v("si", 16, 32), ramp, 0.0, A.add)
    ts(col(9), col(0), 8.0, A.mult, float(PAD), A.add)
    ts(v("q0"), ramp, 0.25, A.mult, col(9), A.add)
    ts(v("il8"), ramp, -0.75, A.mult, col(9), A.add)
    ts(v("Gn32"), v("jg", 0, 128, 16), col(1), A.is_equal)
    cp(v("Gn"), v("Gn32"))
    ts(col(4), col(0), 8.0, A.is_lt); ts(col(5), col(0), 8.0, A.is_ge)
    ts(v("XX", 2 * TW, 2 * TW + 1), col(4), 256.0, A.mult, -1.0, A.add)
    for j, c in enumerate((col(4), col(5), 16.0, 16.0)):
        ts(blk("GM", j, 8), v("Gn32"), c, A.mult)
    ts(v("GE"), v("Gn32"), -512.0, A.mult)
    for j, (c, d) in enumerate(((col(4), -1.0), (col(5), -1.0), (-16.0, 1.0), (496.0, 1.0))):
        ts(blk("YS", j), onh, c, A.mult, d, A.mult)
    ms(v("cV"), 2 * BV)
    ms(v("RS"), 0.0)
    for r in range(4):
        a, n = SEG[r], 16 * (r + 1)
        iota(v("AD", a, a + 2 * n), [[4, 2], [0, n]], r, -1)
        iota(v("sc", a, a + 2 * n), [[0, 2], [1, n]], -16 * r, 0)
        ms(v("sc", 320 + a, 320 + a + 2 * n), 16.0 * r)
        ms(v("RS", a, a + 2 * n, n), float(1 << 25))
    ts(v("SEL"), v("AD", 0, 320), 0.0, A.is_equal, -BIG, A.mult)
    ts(v("sc", 640, 960), v("sc", 0, 320), col(0), A.is_ge, BIG, A.mult)
    ts(v("sc", 960, 1280), v("sc", 320, 640), col(0), A.add, 1.0 / BIG, A.mult)
    tt(v("SEL", 0, 320, 1, 16, 32), v("sc", 640, 960, 1, 16, 32), v("sc", 960, 1280, 1, 16, 32), A.add)
    for j in range(3):
        ts(blk("cT", j, 256), cq, 0.0, A.mult)
        ts(v("cT", 256 * j, 256 * j + 256, 1, 16, 32), v("jk", 0, 256, 1, 16, 32), v("col", 0, 1, 1, 16, 32), A.is_equal, BIG, A.mult)
    for r in range(4):
        a, n = SEG[r], 16 * (r + 1)
        e = v("SEL", a + n - 1, a + 2 * n, n, 8)
        ts(e, e, -1.0 / BIG, A.mult)
        e = v("SEL", a + n - 1, a + 2 * n, n, 16, 32)
        ts(e, e, 0.0, A.mult, (PAD - 1.0) / BIG, A.add)
    ts(v("pi", 3, 4), v("pi", 0, 1), 3, A.bitwise_and)
    ts(v("pi", 4, 5), v("pi", 0, 1), 2, A.arith_shift_right, 1, A.bitwise_and)
    ts(col(6), v("pi", 3, 4), 1.0, A.add, 16.0, A.mult)
    tt(col(7), v("pi", 3, 4), v("pi", 4, 5), A.add)
    ts(col(8), col(7), 1.0, A.add, col(6), A.mult)
    ts(v("ends", 0, 1), col(8), -1.0, A.add)

    for t in range(RO):
        last = t == RO - 1
        z = "zl" if t == 0 else "ys%d" % (t - 1)
        ys, yl, qu, ql, ks, kl, ns, nl, ws, wl = ["%s%d" % (k, t) for k in ("ys", "yl", "qu", "ql", "ks", "kl", "ns", "nl", "ws", "wl")]

        TAG[0] = "P%d" % t
        for (a, b, e) in PG if t else PG0:
            gather(e, v("G16", 16 * a, 16 * b), Pw, v("Rl%d" % t, a, b))
            inturn("g")
        for c in (1, 0):
            a, b = 128 * c, 128 * c + 128
            o = ps(c, 0, 128)
            mms([(o, idh, blk("R1", c))] + [(o, dg(k), v("G16", 16 * a + k, 16 * b, 16)) for k in range(16)])
            relu(ENG["u2"], blk("u2", c), o, -BIG * W)
            ts(blk("Ls", c), o, 1.0 / BIG, A.mult, PAD - 0.2501, A.add)
            mms([(ps(3 + c, 0, 128), M1, blk("u2", c))])
            relu(ENG["u1"], blk("u1", c), ps(3 + c, 0, 128))
            mms([(ps(3 + c, 128, 256), idN4, blk("u2", c)), (ps(3 + c, 128, 256), onh, blk("u1", c))])
            tt(blk("ix", c), ps(3 + c, 128, 256), blk("u2", c), A.max)
            ts(blk("ixu", c), blk("ix", c), PAD - 1.0, A.add)
        ts(v("L1"), v("Ls"), 1.0 - PAD, A.add)
        mms([(ps(6, 0, 256), idb, v(z)), (ps(6, 0, 256), onN, v("u2"))])
        act(v("zz"), ps(6, 0, 256), AF.Relu, scale=2.0)
        TAG[0] = "X%d" % t
        for (a, b, e) in XG if t else XG0:
            gather(e, v("xg", 16 * a, 16 * b), Xw, v("ixu", a, b))
            inturn("x")
            n = 16 * (b - a)
            scan(v("smx", 16 * a, 16 * b), v("rs0", 0, n), v("xg", 16 * a, 16 * b), A.min, A.max)
            scan(v("smn", 16 * a, 16 * b), v("rb", 0, n), v("xg", 16 * a, 16 * b), A.max, A.min)
        if t > 0:
            scatter(XCw, "wl%d" % (t - 1), "nl%d" % (t - 1), DOWN, "cw%d" % t)
        gather(ENG["xq"], v("xq"), XCw, v("q0") if t == 0 else v("qu%d" % (t - 1)))
        o = ps(6, 256, 272)
        mms([(o, idh, v("c256"))] + [(o, v("oto", 15 - k, 143 - k), v("xq", k, 256, 16)) for k in range(16)])
        tt(v("D0", 0, 256, 16), o, v("si", 16, 32), A.max)
        mms([(ps(7, 0, 256), onh, v("xq"))])
        act(v("orow"), ps(7, 0, 256), AF.Relu, bias=1.0, scale=-1.0)

        TAG[0] = "Q%d" % t
        for (a, b), bk in zip(YC, (2, 5)):
            n, a1, b1 = b - a, a // 16, b // 16
            oy, oq = ps(bk, 0, n), ps(bk, 256, 256 + n)
            ends = [v("zz", a, b), v("smx", 16 * a + 15, 16 * b, 16), v("smn", 16 * a + 15, 16 * b, 16)]
            mms([(oy, idb, v("cq", 0, n)), (oq, idb, v("OFF", a, b)), (oq, idb, v("ramp", a, b)), (oq, idb, v("cq", 0, n)), (oq, onB, v("xq", a, b))]
                + [x for r in ends for x in ((oq, s0h, r), (oy, idhalf, r))])
            scan(v("sq", a, b), v("D0", a, b), oq, A.max, A.min)
            ts(v(ys, a, b), oy, MAGIC, A.add, -MAGIC, A.add)
            cp(v("si", a1, b1), v("sq", a + 15, b, 16))
            ts(v("si", 16 + a1, 16 + b1), v("si", a1, b1), 7 + 15 * 512, A.bitwise_and)
            tt(v("qf", a1, b1), v("si", 16 + a1, 16 + b1), v("il8", a1, b1), A.add)
            cp(v(qu, a1, b1), v("qf", a1, b1))
            cp(ind(XCw, v(qu, a1, b1)), v(ys, a, b), chain="cq%d" % t)
        msg(v(ys), DC, v(yl), "my%d" % t)
        msg(v(qu), DC, v(ql), "mq%d" % t)
        if last:
            msg(v(ys), -DB, v("zol"), "mzo")
            dma("sync", T.zo[:], ap(v("zol")), [v("zol")], [], "st")
        for h in (1, 0):
            mms([(ps(6, 0, 128), blk(ys, h), idb)])
            lin("act", blk("yT", h), ps(6, 0, 128), YOFF)
            lin("act", blk("yp", h), blk(ys, h), EOFF)
            mms([(ps(7, 0, 128), id8, blk(ys, h)), (ps(7, 0, 128), ido, blk("orow", h))])
            act(blk("U8", h), ps(7, 0, 128), AF.Abs)
        mms([(ps(6, 0, 256), idh, v("R1")), (ps(6, 0, 256), idb, v("U8"))])
        lin(ENG["RU"], v("RU"), ps(6, 0, 256), BIG)
        if not last:
            ts(v("qh"), v("qf"), -1.0 / BIG, A.mult, (W + PAD) / BIG, A.add)
            for k in range(16):
                mms([(ps(5, 256 + k, 512, 16), dg(k, t), v("qh"))])
            lin(ENG["cap"], v("cap"), ps(5, 256, 512), float(W), -1.0)

        TAG[0] = "E%d" % t
        for (a, b, e) in EG:
            gather(e, v("eg", 16 * a, 16 * b), XCw, v("Ls", a, b), EOFF)
            inturn("e")
        for h in range(2):
            cp(ind(Xw, blk(ql, h, 8)), blk(yl, h))
        for h in (1, 0):
            TAG[0] = "E%d%d" % (t, h)
            bk = 4 - h
            s0, s32, s1, s8 = [blk("st", 4 * h + j) for j in range(4)]
            R1, L1 = blk("R1", h), blk("L1", h)
            ba = 2 if h else 7
            mms([(ps(ba, 0, 256), blk("yp", h), v("YS", 0, 256))], stop=False)
            mms([(ps(bk, 256, 512), blk("yp", h), v("YS", 256, 512)), (ps(bk, 384, 512), idb, v("cV"))]
                + [(ps(bk, 384 + k, 512, 16), v("eg", 2048 * h + k, 2048 * h + 2048, 16), v("GE")) for k in range(16)], stop=False)
            for j in range(4):
                mms([(ps(j % 2), blk("yT", h), blk("EX", j, 512))])
                tt(blk("Mx", 4 * h + j, 512), blk("eg", 4 * h + j, 512), ps(j % 2), A.max)
            mms([(ps(ba, k, 256, 16), v("Mx", 2048 * h + k, 2048 * h + 2048, 16), v("GM", 0, 16)) for k in range(16)], start=False)
            mms([(ps(bk, 256 + k, 512, 16), v("Mx", 2048 * h + k, 2048 * h + 2048, 16), v("GM", 16, 32)) for k in range(16)], False, False)
            ts(blk("Pr", h, 256), ps(ba, 0, 256), MAGIC, A.add, -MAGIC, A.add)
            mms([(ps(bk, 256, 384), idn16, blk("Pr", 2 * h)), (ps(bk, 256, 384), idn16, blk("Pr", 2 * h + 1)),
                 (ps(bk, 384, 512), id1008, blk("Pr", 2 * h)), (ps(bk, 384, 512), id1008, blk("Pr", 2 * h + 1))], start=False)
            act(blk("tB", h), ps(bk, 256, 384), AF.Abs, bias=8.5 * BV, scale=BV)
            tt(blk("km", h), ps(bk, 384, 512), blk("tB", h), A.min)
            scan(blk("S", h), v("pot"), blk("km", h), A.add, A.max)
            ts(v("si", 32 + 8 * h, 40 + 8 * h), v("S", 128 * h + 15, 128 * h + 128, 16), 17.0 - 2 * BV, A.add, 0.0, A.max)
            ts(v("si", 48 + 8 * h, 56 + 8 * h), v("si", 32 + 8 * h, 40 + 8 * h), 511, A.bitwise_and)
            ts(v("sp", 128 * h, 128 * h + 128, 16), v("si", 48 + 8 * h, 56 + 8 * h), -480.0, A.add)
            scan(blk("rep", h), v("rs0", 0, 128), blk("sp", h), A.min, A.add)
            for o, c in ((s0, 0.0), (s32, 32.0), (s1, 1.0), (s8, 8.0)):
                ts(o, blk("rep", h), c, A.is_ge)

            TAG[0] = "T%d%d" % (t, h)
            for j in ((1, 0) if last else (0, 1)):
                bK, bT, bD = (((1, 4, 7), (0, 0, 2)), ((5, 3, 2), (6, 5, 5)))[h][j]
                u = 2 * h + j
                K, cT, o = blk("KK", u), v("cT", 128 * u, 128 * u + 128, 1, 8), ps(bK, 0, 128)
                mms([(o, idh, (R1, L1)[j]), (o, (s0, s1)[j], idB8), (o, (s32, s8)[j], idN8)])
                relu(ENG["K"][u], K, o, -BIG8)
                for m in range(16):
                    mms([(ps(bT, 128 + m, 256, 16, 8), v("KK", 128 * u + m, 128 * u + 128, 16), v("Gn"))])
                lin(ENG["cT"][u], cT, ps(bT, 128, 256, 1, 8))
                if j == 0:
                    mms([(ps(bk, 256, 264), cT, v("idh", 0, 8, 1, 8))])
                    if not last:
                        o = ps(bk, 384, 512)
                        mms([(o, idb, v("MB", t, t + 128)), (o, s1, idB8), (o, s32, idN8)], stop=False)
                    ts(v("tl", 8 * h, 8 * h + 8), ps(bk, 256, 264), PAD - 1.0, A.add)
                rows = [(ps(bD, SEG[r] + 16 * (r + 1) * q, SEG[r] + 16 * (r + 1) * (q + 1) - 1), onB,
                         v("KK", 128 * u + 64 * q, 128 * u + 64 * q + 16 * r + 15)) for r in range(4) for q in range(2)]
                o = ps(bD, 0, 320)
                if h:
                    mms([(o, v("cT", 128 * u, 128 * u + 128, 1, 48), v("SEL", 0, 320, 1, 48))] + rows)
                else:
                    mms([(o, v("cT", 512, 640, 1, 48), v("SEL", 0, 320, 1, 48))] + rows + [(o, cT, v("SEL", 0, 320, 1, 8))])
                act(blk("AD", u, 320), o, AF.Abs)
                scan(blk("sc", u, 320), v("RS"), blk("AD", u, 320), A.add, A.min)
                cp(blk((ws, ks)[j], h, 16), ind(blk("sc", u, 320), v("ends", 0, 1)))
            if not last:
                gather(ENG["oP"], blk("oP", h), Pw, v("tl", 8 * h, 8 * h + 8))
                mms([(ps(bk, 384, 512), idh, blk("oP", h))], start=False)
                tt(blk("nP", h), ps(bk, 384, 512), blk("cap", h), A.min)
            od, ou = ps(5, 384, 512), ps(6, 128, 256)
            mms([(ou, idh, L1), (ou, idb, blk("U8", h)), (ou, s8, idB8), (ou, s32, idN8)])
            tt(blk("vi", h), ou, blk("RU", h), A.max)
            ts(blk("vj", h), blk("vi", h), W - 1, A.bitwise_and)
            if not last:
                ts(blk("Rl%d" % (t + 1), h), blk("vj", h), float(PAD), A.add)
            mms([(od, idh, L1), (od, idhn, R1), (od, s8, idB8), (od, s32, idN8)])
            relu("act", blk("D32", h), od, TW - BIG8)
            lin("act", blk("Rf", h) if last else R1, blk("vj", h), 0.0 if last else 1.0)
            for m in range(16):
                o = ps(bk, m, 128, 16, 8)
                mms([(o, v("KK", 256 * h + m, 256 * h + 128, 16), v("Gn")), (o, v("D32", 128 * h + m, 128 * h + 128, 16), v("Gn32"))])
            cT3 = v("cT3", 128 * h, 128 * h + 128, 1, 8)
            lin("act", cT3, ps(bk, 0, 128, 1, 8))
            mms([(ps(bk, 256, 264), cT3, v("id32", 0, 8, 1, 8))])
            ts(v("tl", 16 + 8 * h, 24 + 8 * h), ps(bk, 256, 264), PAD - 1.0, A.add)

        TAG[0] = "S%d" % t
        if not last:
            scatter(Pw, ws, "nP", DOWN, "p%d" % t)
        for h in (1, 0):
            msg(v(ks, 16 * h, 16 * h + 8), DC, v(kl, 16 * h, 16 * h + 8), "m%s%d" % ("kj"[h], t))
        if last:
            msg(v("Rf"), -DB, v("rol"), "mro")
            dma("sync", T.ro[:], ap(v("rol")), [v("rol")], [], "st")
        else:
            msg(v(ws), -DC, v(wl), "mw%d" % t)
        scatter(Xw, kl, None, DOWN, "xk%d" % t)
        for j in range(2):
            gather(ENG["oX"][j], blk("oX", j, 256), XX, blk("tl", j, 16))
        if not last:
            scatter(XCw, ks, None, DOWN, "ck%d" % t)
        o = ps(7, 256, 512)
        mms([(o, idb, cq), (o, idhalf, v("oX", 256, 512)), (o, idhalf, v("oX", 0, 256))])
        ts(v(ns), o, MAGIC, A.add, -MAGIC, A.add)
        scatter(Xw, ws, ns, DOWN, "xw%d" % t)
        if not last:
            msg(v(ns), -DC, v(nl), "mn%d" % t)

    dma("sync", T.xo[:, 0:1024], ap(v("XX", PAD, PAD + 1024)), [Xw], [], "st")
    dma("act", T.xo[:, 1024:2048], ap(v("XX", PAD + 1024, TW)), [Xw], [], "st")

    n = len(ops)
    succ = [[] for _ in range(n)]
    left = [0] * n
    for k, o in enumerate(ops):
        pre = set(o["deps"]) | set(o["order"])
        left[k] = len(pre)
        for j in pre:
            succ[j].append(k)
    prio = [0.0] * n
    for k in range(n - 1, -1, -1):
        o = ops[k]
        prio[k] = o["cost"] + o.get("first", 0.0) + max([0.0] + [prio[j] + (o["lat"] + HOP if k in ops[j]["deps"] else 0.0) for j in succ[k]])
    pred = [[(j, ops[j]["lat"] + HOP if j in o["deps"] else 0.0) for j in set(o["deps"]) | set(o["order"])] for o in ops]
    post = [[(j, ops[k]["lat"] + HOP if k in ops[j]["deps"] else 0.0) for j in succ[k]] for k in range(n)]

    def place(order, before, tail):
        end = [0.0] * n
        busy = {}
        for k in order:
            o = ops[k]
            s = max([tail[k]] + [end[j] + d for j, d in before[k]])
            if o["q"] != "land":
                b = busy.setdefault(o["q"], [])
                i = len(b)
                while i > 0 and b[i - 1][1] > s:
                    i -= 1
                while i < len(b) and b[i][0] < s + o["cost"]:
                    s = max(s, b[i][1])
                    i += 1
                b.insert(i, (s, s + o["cost"]))
            end[k] = s + o["cost"]
        return end

    if not ORDER:
        order = sorted(range(n), key=lambda k: (-prio[k], k))
        best = None
        for _ in range(SWEEPS):
            end = place(order, pred, [0.0] * n)
            span = max(end[k] + ops[k]["lat"] for k in range(n))
            SPAN.append(round(span))
            if best is None or span < best:
                best = span
                ORDER[:] = sorted(range(n), key=lambda k: (end[k] - ops[k]["cost"], k))
            back = place(sorted(range(n), key=lambda k: (-end[k], -k)), post, [o["lat"] for o in ops])
            order = sorted(range(n), key=lambda k: (-back[k], k))
        seed = [1]

        def draw(m):
            seed[0] = (seed[0] * 1103515245 + 12345) % 2147483648
            return (seed[0] >> 8) % m
        end = place(ORDER, pred, [0.0] * n)
        key = [end[k] - ops[k]["cost"] for k in range(n)]
        for _ in range(SHAKES):
            amp, mid, wide = (100, 300, 1000, 3000)[draw(4)], draw(int(best)), (3000, 10000, 40000)[draw(3)]
            k2 = [x + (draw(2 * amp) - amp if abs(x - mid) < wide and draw(10) < 3 else 0) for x in key]
            for k in range(n):
                k2[k] = max([k2[k]] + [k2[j] for j, d in pred[k]])
            end = place(sorted(range(n), key=lambda k: (k2[k], k)), pred, [0.0] * n)
            back = place(sorted(range(n), key=lambda k: (-end[k], -k)), post, [o["lat"] for o in ops])
            end = place(sorted(range(n), key=lambda k: (-back[k], k)), pred, [0.0] * n)
            span = max(end[k] + ops[k]["lat"] for k in range(n))
            if span <= best:
                best = span
                key = [end[k] - ops[k]["cost"] for k in range(n)]
                ORDER[:] = sorted(range(n), key=lambda k: (key[k], k))
                SPAN.append(round(span))
    seq = ORDER
    pos = {k: i for i, k in enumerate(seq)}
    need = set()
    for o in ops:
        best = {}
        for j in o["deps"]:
            if ops[j]["tok"] is None and pos[j] > pos.get(best.get(ops[j]["q"]), -1):
                best[ops[j]["q"]] = j
        o["deps"] = [j for j in sorted(o["deps"]) if ops[j]["tok"] is not None] + sorted(best.values())
        need.update(best.values())
    eng = {"dve": g.vector, "act": g.scalar, "pe": g.tensor, "pool": g, "sync": g.sync}
    seen = {q: {} for q in eng}
    toks = {}
    for k in seq:
        o = ops[k]
        q = o["q"]
        if o["tok"] is not None:
            toks[k] = o["tok"]
        if q == "land":
            continue
        for j in o["deps"]:
            sem, val = toks[j]
            if seen[q].get(sem, 0) < val:
                eng[q].wait_ge(T.sem[sem], val)
                seen[q][sem] = val
        TAG[0] = o["tag"]
        r = o["fn"]()
        if k in need:
            total[q] = total.get(q, 0) + 1
            r.then_inc(T.sem[q], 1)
            toks[k] = (q, total[q])
    for sem in SEMAPHORES:
        if total.get(sem, 0) and max(seen[q].get(sem, 0) for q in seen) < total[sem]:
            g.wait_ge(T.sem[sem], total[sem])
